import numpy as np, ml_dtypes
CORES = [25,29,65,69,153,157,193,197]
N = 8
BF = ml_dtypes.bfloat16
def gentries(a):
    return np.ascontiguousarray(a.reshape(8, 16, -1).transpose(0, 2, 1)).reshape(8, -1)
def gtable(e):
    e = np.asarray(e); return np.ascontiguousarray(e.reshape(8, -1, 16).transpose(0, 2, 1)).reshape(128, -1).astype(np.int32)
V, K, A, B, R = 1536, 5, 5, 4, 3
LR = V // R
LOW = 0.0625
def parts(rng):
    s = LOW + (1.0 - LOW) * rng.random((N, 8, 16, V)); nb = rng.integers(0, V, (N, 8, R, K, LR))
    tr = np.where(rng.random((N, 8, 1, V)) < 0.5, rng.integers(1, 16, (N, 8, K, V)), rng.integers(10, 16, (N, 8, K, V)))
    return s, nb, tr, rng.integers(0, V, (N, 8, V)), rng.integers(0, V, (N, 8, V))
def kinds(rng, n):
    return (np.arange(N)[:, None] + np.arange(8) + rng.integers(0, n)) % n
def pack(s, nb, tr, ex, pt):
    return {"sat": np.clip(s.reshape(N, 128, V).astype(np.float32), np.float32(LOW), np.float32(1)), "nb": np.stack([gtable(a.reshape(8, -1)) for a in nb]),
            "tr": np.ascontiguousarray(tr.reshape(N, 8 * K, V)).astype(np.float32).astype(BF), "ex": np.ascontiguousarray(ex).astype(np.int32), "pt": np.ascontiguousarray(pt).astype(np.int32)}
def setup_inputs(rng):
    return pack(*parts(rng))
def setup_inputs_spread(rng):
    s, nb, tr, ex, pt = parts(rng)
    s = np.exp2(-4.0 * rng.random((N, 8, 1, V))) * (0.5 + 0.5 * rng.random((N, 8, 16, V)))
    tr = np.minimum(np.floor(np.exp2(4.0 * rng.random(tr.shape))), 15).astype(np.int64)
    nb = np.minimum((V * rng.random(nb.shape) ** 3).astype(np.int64), V - 1); nb[:, 1::2] = V - 1 - nb[:, 1::2]
    ex = np.minimum((V * rng.random(ex.shape) ** 2).astype(np.int64), V - 1); pt = V - 1 - np.minimum((V * rng.random(pt.shape) ** 2).astype(np.int64), V - 1)
    return pack(s, nb, tr, ex, pt)
def tips(rng, a):
    return np.where(rng.random(a.shape) < 0.75, (V - 1) * rng.integers(0, 2, a.shape), a)
def setup_inputs_ends(rng):
    s, nb, tr, ex, pt = parts(rng); nb = tips(rng, nb); ex = tips(rng, ex); pt = tips(rng, pt); tr = 1 + 14 * rng.integers(0, 2, tr.shape)
    s = np.where(rng.random((N, 8, 1, V)) < 0.75, np.where(rng.random(s.shape) < 0.5, LOW, 1.0), s)
    for c in (0, V - 1):
        s[:, :, 12:, c] = 1.0; s[:, :, :4, c] = LOW; s[:, :, 4:12, c] = np.where(rng.random((N, 8, 8)) < 0.5, LOW, 1.0)
        ex[:, :, c] = (V - 1) * rng.integers(0, 2, (N, 8)); pt[:, :, c] = (V - 1) * rng.integers(0, 2, (N, 8))
        nb[:, :, c // LR, :, c % LR] = (V - 1) * rng.integers(0, 2, (N, 8, K))
    nb[N - 1, 7, R - 1, 1, LR - 1] = 0; nb[N - 1, 7, R - 1, K - 1, LR - 1] = V - 1
    tr[N - 1, 7, :, V - 1] = 1; tr[N - 1, 7, 1, V - 1] = 15; tr[N - 1, 7, K - 1, V - 1] = 15
    tr[N - 1, 7, :, V - 2] = 1; tr[N - 1, 7, K - 1, V - 2] = 15
    return pack(s, nb, tr, ex, pt)
def setup_inputs_corners(rng):
    s, nb, tr, ex, pt = parts(rng); kd = kinds(rng, 4)
    s[:, :, 1:8] = s[:, :, :1]; s[:, :, 9:] = s[:, :, 8:9]; s[..., V - LR + 1::2] = s[..., V - LR::2]
    m = kd == 0; own = np.arange(V).reshape(R, 1, LR)
    nb[m] = np.where(np.arange(K)[:, None] % 2 == 0, own, rng.choice(np.array([0, V - 2, V - 1]), nb[m].shape)); ex[m] = np.arange(V); pt[m] = rng.choice(np.array([0, V - 1]), pt[m].shape)
    m = kd == 1; n = nb[m].shape[0]
    nb[m] = V - 1 - rng.integers(0, 4, nb[m].shape); ex[m] = np.where(rng.random((n, V)) < 0.5, V - 1 - rng.integers(0, 4, (n, V)), ex[m])
    pt[m] = V - 1 - rng.integers(0, 2, (n, V)); tr[m] = 1 + 14 * rng.integers(0, 2, (n, 1, V))
    m = kd == 2; v = nb[m]; v[:, :, 0:K - 1:2] = rng.integers(V - LR, V, v[:, :, 0:K - 1:2].shape); v[:, :, 1::2] = v[:, :, 0:K - 1:2] ^ 1
    nb[m] = v; tr[m] = 1 + 14 * rng.integers(0, 2, (v.shape[0], 1, V))
    m = kd == 3; ex[m] = (np.arange(V) + 1) % V; pt[m] = rng.choice(np.array([0, 1, V - 2, V - 1]), pt[m].shape)
    n = nb[m].shape[0]; e = V - LR + 2 * rng.integers(0, LR // 2, n); sm = s[m]; sm[np.arange(n), :, e] = 1.0; sm[np.arange(n), :, e + 1] = 0.5; s[m] = sm
    kk = np.arange(K)[:, None]; j = rng.integers(0, K, (n, 1, V)); i = (j + 1 + rng.integers(0, K - 1, (n, 1, V))) % K; hit = (rng.random((n, 1, V)) < 0.5) & (np.arange(V) < V - LR)
    v = nb[m].transpose(0, 2, 1, 3).reshape(n, K, V); v = np.where(hit & (kk == j), e[:, None, None], np.where(hit & (kk == i), e[:, None, None] + 1, v))
    nb[m] = v.reshape(n, K, R, LR).transpose(0, 2, 1, 3)
    tr[m] = np.where(hit, np.where(kk == j, 3, np.where(kk == i, 8, rng.integers(1, 3, (n, K, V)))), tr[m])
    return pack(s, nb, tr, ex, pt)
def setup_inputs_crowd(rng):
    s, nb, tr, ex, pt = parts(rng); kd = kinds(rng, 4); p = int(rng.integers(1, 16)); odd = s[:, :, p].copy()
    s[:, :, 1:] = s[:, :, :1].copy(); s[:, :, p] = odd
    m = kd == 0; n = nb[m].shape[0]; nb[m] = rng.integers(0, V, (n, 1, 1, 1)); pt[m] = rng.integers(0, V, (n, 1))
    m = kd == 1; n = nb[m].shape[0]; few = rng.integers(0, V, (n, 4))
    nb[m] = few[np.arange(n)[:, None, None, None], rng.integers(0, 4, (n, R, K, LR))]; tr[m] = rng.integers(1, 16, (n, 1, V))
    m = kd == 2; n = nb[m].shape[0]; j = rng.integers(0, K, (n, 1, V)); kk = np.arange(K)[:, None]; tr[m] = np.where(kk == j, 15, 1)
    m = kd == 3; n = nb[m].shape[0]; j = rng.integers(0, K, (n, 1, V)); i = (j + 1 + rng.integers(0, K - 1, (n, 1, V))) % K; tr[m] = np.where((kk == j) | (kk == i), 15, 1)
    return pack(s, nb, tr, ex, pt)
THIRD = (11183600, 11183900, 2048, -25)
BANDS = ((2 ** 23, 2 ** 24 - 16, 16, -27), (2 ** 23, 2 ** 24 - 16, 16, -26), THIRD, THIRD, THIRD, (13421773, 2 ** 24 - 8, 8, -25), (2 ** 23, 2 ** 24 - 2 ** 20, 4, -24), (15770584, 2 ** 24 - 4, 4, -24))
def setup_inputs_calm(rng):
    s, nb, tr, ex, pt = parts(rng); kd = kinds(rng, 2)
    for p, (lo, hi, wd, e) in enumerate(BANDS): s[:, :, p] = (rng.integers(lo, hi) + rng.integers(0, wd, (N, 8, V))) * 2.0 ** e
    tr[:] = rng.integers(1, 16, (N, 8, 1, V))
    m = kd == 0; n = nb[m].shape[0]; nb[m] = rng.integers(0, 4, nb[m].shape)
    ex[m] = np.where(rng.random((n, V)) < 0.5, rng.integers(0, 4, (n, V)), ex[m]); pt[m] = np.where(rng.random((n, V)) < 0.5, rng.integers(0, 4, (n, V)), pt[m])
    return pack(s, nb, tr, ex, pt)
def check_inputs(d):
    bad = []
    for k, lo, hi in (("sat", LOW, 1), ("nb", 0, V - 1), ("tr", 1, 15), ("ex", 0, V - 1), ("pt", 0, V - 1)):
        a = np.asarray(d[k]).astype(np.float64)
        if not (np.min(a) >= lo and np.max(a) <= hi): bad.append("range of " + k)
        elif k == "tr" and np.any(a != np.floor(a)): bad.append("whole numbers in " + k)
    return bad
ONE, TWO, THREE, HALF = np.float32(1), np.float32(2), np.float32(3), np.float32(0.5)
def flow(s):
    return (s * s) * (THREE - TWO * s)
def step(y, s):
    return s + HALF * (flow(y) - flow(s))
def pick(w, ix):
    return np.take_along_axis(w, ix[:, :, None, :], 3)
def reference(sat, nb, tr, ex, pt):
    s = sat.astype(np.float32).reshape(N, 8, 16, V); x = ex.astype(np.int64); po = pt.astype(np.int64)
    cand = np.stack([gentries(a) for a in nb]).astype(np.int64).reshape(N, 8, R, K, LR); w = tr.astype(np.float32).reshape(N, 8, K, R, LR)
    for t in range(R):
        lo = t * LR
        c = [np.zeros((N, 8, 1), np.int64) + np.arange(lo, lo + LR)]
        for j in range(A - 1): c.append(np.take_along_axis(x, c[-1], 2))
        sf = np.roll(s, (-1, -t), (0, 1)); xf = np.roll(x, (-1, -t), (0, 1))
        d = [np.take_along_axis(po, c[-1], 2)]
        for j in range(B - 1): d.append(np.take_along_axis(xf, d[-1], 2))
        y = pick(sf, d[B - 1])
        for j in range(B - 2, -1, -1): y = step(y, pick(sf, d[j]))
        for j in range(A - 1, -1, -1): y = step(y, pick(s, c[j]))
        s[..., lo:lo + LR] = y
        n = cand[:, :, t]
        u = pick(s, n.reshape(N, 8, K * LR)).reshape(N, 8, 16, K, LR)
        v = ONE - u
        q = w[:, :, :, t][:, :, None] * (u * u + HALF * (v * v))
        k = np.argmax(q, axis=3)
        votes = np.sum((k[:, :, :, None, :] == np.arange(K)[:, None]).astype(np.int64), axis=2)
        win = np.argmax(votes, axis=2)
        x[..., lo:lo + LR] = np.take_along_axis(n, win[:, :, None], 2)[:, :, 0]
    return {"ys": s.reshape(N, 128, V), "yx": x.astype(np.float32)}

@@ -1,0 +1,755 @@
+from concourse.bass import DstId, RemoteDMATransfer
+from concourse.mybir import AluOpType as ALU, ActivationFunctionType as ACT
+
+V, LR, R = 1536, 512, 3
+F32, I32, U16, F16, BF = "float32", "int32", "uint16", "float16", "bfloat16"
+SCRATCH = {
+    "S": ("sbuf", [128, V], F32), "NG": ("sbuf", [128, V], F32), "Q": ("sbuf", [128, V], F32),
+    "SF0": ("sbuf", [128, V], F32), "SF1": ("sbuf", [128, V], F32), "SF2": ("sbuf", [128, V], F32),
+    "GF0": ("sbuf", [128, V], F32), "GF1": ("sbuf", [128, V], F32), "GF2": ("sbuf", [128, V], F32),
+    "K": ("sbuf", [128, V], BF), "E": ("sbuf", [128, V], BF), "XF": ("sbuf", [128, V], BF),
+    "CM": ("sbuf", [128, 288], I32), "LO": ("sbuf", [128, 288], I32), "HB": ("sbuf", [128, 576], BF),
+    "D1": ("sbuf", [128, 7 * V], F32), "D0": ("sbuf", [128, V], F32), "D0F": ("sbuf", [128, V // 2], F32),
+    "Y": ("sbuf", [128, V], F32),
+    "LS1": ("sbuf", [128, LR], F32), "LS2": ("sbuf", [128, LR], F32),
+    "LW1": ("sbuf", [128, 32], U16), "LW2": ("sbuf", [128, 32], U16), "LX": ("sbuf", [128, 192], BF),
+    "QG": ("sbuf", [128, 5 * LR], F32), "M": ("sbuf", [128, 4 * LR], F32), "AV": ("sbuf", [128, 4 * LR], BF),
+    "HL": ("sbuf", [128, LR], F32), "VL": ("sbuf", [128, LR], F32), "SQ": ("sbuf", [128, LR], F32),
+    "GH": ("sbuf", [128, 2 * LR], BF), "OFF": ("sbuf", [128, 7 * 32], U16),
+    "EXT": ("sbuf", [128, 3, 32], I32), "EXF": ("sbuf", [128, 96], F32),
+    "EXG": ("sbuf", [128, 96], F32), "EXW": ("sbuf", [128, 96], U16),
+    "NB": ("sbuf", [128, 3, 160], I32), "NBW": ("sbuf", [128, 480], U16), "CODE": ("sbuf", [128, 3, 160], F32),
+    "TR": ("sbuf", [40, V], BF), "ONE": ("sbuf", [40, 640], BF), "WS": ("sbuf", [40, 640], BF),
+    "DZ": ("sbuf", [128, 144], F32), "PC": ("sbuf", [128, 4], I32), "PF": ("sbuf", [128, 12], F32),
+    "ZB": ("sbuf", [128, 144], BF), "Z": ("sbuf", [128, 4 * 144], BF),
+    "D2": ("sbuf", [128, 160], I32), "I2": ("sbuf", [128, 160], F16),
+    "MX": ("sbuf", [128, 96], F32), "MI": ("sbuf", [128, 64], I32), "NW": ("sbuf", [128, 32], U16),
+    "XH": ("sbuf", [128, 32], F16), "RU1": ("sbuf", [128, 32], U16), "RU2": ("sbuf", [128, 32], U16),
+    "XO": ("sbuf", [128, 32], F32), "XT": ("sbuf", [128, 96], F32),
+    "PS": ("psum", [128, 8 * LR], F32),
+}
+MSGS = ["X0", "S0a", "S0b", "S0c", "S1", "W1", "S2", "W2"]
+NDMA = 40
+SEMAPHORES = ["cV", "cA", "cP", "cG"] + ["a" + m for m in MSGS] + ["l" + m for m in MSGS] + ["d%d" % i for i in range(NDMA)]
+
+CYC = 0.83e-3
+PARS = [
+    {"f": 1.25, "g": 1.55, "pe": 0.6e-3, "sy": 0.06, "dl": 2.0, "rl": 1.0, "add": 1},
+    {"f": 1.1, "g": 1.95, "pe": 0.5e-3, "sy": 0.1, "dl": 1.5, "rl": 1.3, "add": 1},
+    {"f": 1.35, "g": 1.15, "pe": 1.0e-3, "sy": 0.04, "dl": 2.3, "rl": 0.8, "add": 0},
+]
+PAR = dict(PARS[0])
+OPT = {"LH": 1, "SPLIT": 2, "STEPS": 5000, "SEED": 5, "PASS": 100, "AMP": 1.2, "PEN": 1.5, "LNS": 4500}
+
+
+def tv(n, c=1.0, f0=0.055):
+    x = n * c * CYC
+    return PAR["f"] * (f0 + x if PAR["add"] or c == PAR["g"] else max(f0, x))
+
+
+def ta(n, c=1.0):
+    return tv(n, c, 0.065)
+
+
+def message(T, m):
+    if m == "X0":
+        return T.HB, 0, T.LX, 0, 192, False
+    if m[0] == "W":
+        return T["RU" + m[1]], 0, T["LW" + m[1]], 0, 32, False
+    if m[1] == "0":
+        b = "abc".index(m[2])
+        return T.S, b * LR, T.SF0, b * LR, LR, True
+    return T.S, (int(m[1]) - 1) * LR, T["LS" + m[1]], 0, LR, True
+
+
+def bits(mask):
+    return bin(mask).count("1")
+
+
+def helpers(T, topo, src, dst):
+    hs = [c for c in topo.cores_of(src) if T.rank_of(c) is None and topo.may_write(c, dst)]
+    return sorted(hs, key=lambda c: (topo.die(c) != topo.die(src), c))
+
+
+def parts(topo, src, h, n):
+    es = topo.engines(src, h)
+    k = len(es) // n
+    return [sum(1 << e for e in es[i * k:(i + 1) * k]) for i in range(n)]
+
+
+def arrivals(T, topo, src, dst, wide):
+    if topo.may_write(src, dst):
+        return bits(topo.mask(src, dst))
+    hs = helpers(T, topo, src, dst)
+    return sum(bits(topo.mask(h, dst)) for h in (hs if wide else hs[:1]))
+
+
+def send(g, T, topo, src, dst, m):
+    sb, so, lb, lo, n, wide = message(T, m)
+    if topo.may_write(src, dst):
+        rid, pid = topo.addr(dst, src)
+        g.remote_dma(lb[:, lo:lo + n], sb[:, so:so + n], T.sem["a" + m], T.sem["l" + m], pid, rid, topo.mask(src, dst))
+        return bits(topo.mask(src, dst))
+    hs = helpers(T, topo, src, dst)
+    if not wide:
+        rid, pid = topo.addr(hs[0], src)
+        g.remote_dma(lb[:, lo:lo + n], sb[:, so:so + n], T.sem["a" + m], T.sem["l" + m], pid, rid, topo.mask(src, hs[0]))
+        return bits(topo.mask(src, hs[0]))
+    w = n // len(hs)
+    ms = parts(topo, src, hs[0], len(hs))
+    trs = []
+    for i, h in enumerate(hs):
+        rid, pid = topo.addr(h, src)
+        trs.append(RemoteDMATransfer(dst_ids=[DstId(rid=rid, pnc=pid)], dma_engine_mask=ms[i], remote_sem=T.sem["a" + m],
+                                     src=sb[:, so + i * w:so + (i + 1) * w], dst=lb[:, lo + i * w:lo + (i + 1) * w]))
+    g.remote_dma_fused(trs, local_sem=T.sem["l" + m])
+    return sum(bits(x) for x in ms)
+
+
+def helper_program(g, core, T, topo):
+    n = len(T.cores)
+    for r in range(n):
+        src, dst = T.cores[r], T.cores[(r - 1) % n]
+        if topo.may_write(src, dst):
+            continue
+        hs = helpers(T, topo, src, dst)
+        if core not in hs:
+            continue
+        i = hs.index(core)
+        rid, pid = topo.addr(dst, core)
+        mask = topo.mask(core, dst)
+        sent = []
+        for m in MSGS:
+            sb, so, lb, lo, w, wide = message(T, m)
+            if wide:
+                w = w // len(hs)
+                lo = lo + i * w
+                got = bits(parts(topo, src, hs[0], len(hs))[i])
+            elif i == 0:
+                got = bits(topo.mask(src, core))
+            else:
+                continue
+            g.wait_ge(T.sem["a" + m], got)
+            g.remote_dma(lb[:, lo:lo + w], lb[:, lo:lo + w], T.sem["a" + m], T.sem["l" + m], pid, rid, mask)
+            sent.append(m)
+        for m in sent:
+            g.wait_ge(T.sem["l" + m], bits(mask))
+
+
+def build(T):
+    ops = []
+
+    def op(eng, dur, rd, wr, fn, lat=0.0, kind="c", extra=None):
+        ops.append({"eng": eng, "dur": dur, "rd": rd, "wr": wr, "fn": fn, "lat": lat, "kind": kind, "x": extra})
+
+    def vec(n, c, rd, wr, fn):
+        op(["V"], {"V": tv(n, c)}, rd, wr, fn)
+
+    def act(n, rd, wr, out, in_, func, bias=0.0, scale=1.0):
+        def fn(q, e):
+            if e == "A":
+                return q.activation(out, in_, func, bias=bias, scale=scale)
+            if func == ACT.Square:
+                return q.tensor_tensor(out, in_, in_, ALU.mult)
+            return q.tensor_scalar(out, in_, scale, bias, ALU.mult, ALU.add)
+        both = func == ACT.Identity or bias == 0.0
+        op(["A", "V"] if both else ["A"], {"A": ta(n), "V": tv(n, 2 if func == ACT.Square else 1)}, rd, wr, fn)
+
+    def dma(rd, wr, pairs, nbytes, eng="S", first=False):
+        op([eng], {eng: 0.1 * len(pairs)}, rd, wr, pairs, lat=PAR["dl"] + nbytes / 2.5e5, kind="d", extra=first)
+
+    def pool(dur, rd, wr, fn):
+        op(["G"], {"G": dur * PAR["f"]}, rd, wr, fn)
+
+    def fill(ap, x, n, wr, fl, c=1.0):
+        def fn(q, e):
+            if e == "V":
+                return q.memset(ap, float(x))
+            return q.iota(ap, [[0, n]], int(x), 0, allow_small_or_imprecise_dtypes=True)
+        op(["V", "G"], {"V": tv(n, c), "G": PAR["f"] * (0.13 + 2 * n * CYC)}, [], wr, fn)
+
+    def snd(m, rd, lat):
+        op(["G"], {"G": 2.3 if m == "X0" else 0.3}, rd, ["sent" + m, "order"], None, lat=0.0, kind="s", extra=m)
+        op([], {}, ["sent" + m], ["L" + m], None, lat=(1.5 + lat) * PAR["rl"], kind="a", extra=m)
+
+    def bank(b, a=0, n=LR):
+        return T.PS[:, b * LR + a:b * LR + a + n]
+
+    def blk(t, b, a=0, n=LR):
+        return t[:, b * LR + a:b * LR + a + n]
+
+    def tt(out, a, b, o, rd, wr, n, c=1.0):
+        vec(n, c, rd, wr, lambda q, e: q.tensor_tensor(out, a, b, o))
+
+    def ts(out, a, s, o, rd, wr, n, c=1.0):
+        vec(n, c, rd, wr, lambda q, e: q.tensor_scalar(out, a, s, None, o))
+
+    def cp(out, a, rd, wr, n, c=1.0):
+        vec(n, c, rd, wr, lambda q, e: q.tensor_copy(out, a))
+
+    def rot(dst, dc, src, sc, n, t):
+        s = 16 * t
+        return [(dst[0:128 - s, dc:dc + n], src[s:128, sc:sc + n]), (dst[128 - s:128, dc:dc + n], src[0:s, sc:sc + n])]
+
+    def all3(k):
+        return [k + "0", k + "1", k + "2"]
+
+    dma([], ["CM0"], [(T.CM[:, 0:96], T.ex[:, :])], 5e4, eng="A", first=True)
+    dma([], ["EXT"], [(T.EXT[:, :, 16 * q:16 * q + 16], T.ex[q::2, :]) for q in (0, 1)], 1e5, first=True)
+    dma([], ["CM1"], [(T.CM[:, 96:192], T.pt[:, :])], 1e5, eng="A", first=True)
+    for b in range(3):
+        dma([], ["S%d" % b], [(blk(T.S, b), blk(T.sat, b))], 2.6e5 * (b + 1), eng="ASS"[b], first=True)
+    pool(0.13 + 192 * CYC, [], ["CM2"], lambda q, e: q.iota(T.CM[:, 192:288], [[1, 96]], 0, 0))
+    pool(0.14, [], ["PC0"], lambda q, e: q.iota(T.PC[:, 0:1], [[1, 1]], 0, 1))
+    ts(T.PC[:, 1:2], T.PC[:, 0:1], 15, ALU.bitwise_and, ["PC0"], ["PC1"], 1)
+    cp(T.PF[:, 0:1], T.PC[:, 1:2], ["PC1"], ["PF0"], 1)
+    ts(T.PF[:, 8:9], T.PC[:, 1:2], 96.0, ALU.mult, ["PC1"], ["PF8"], 1)
+    ts(T.CM[:, 192:288], T.CM[:, 192:288], T.PF[:, 8:9], ALU.add, ["CM2", "PF8"], ["CM2"], 96)
+    vec(V, 0.5, [], ["K"], lambda q, e: q.memset(T.K[:, :], 0.0))
+    for x in range(3):
+        a, lo = T.CM[:, 96 * x:96 * x + 96], T.LO[:, 96 * x:96 * x + 96]
+        ts(lo, a, 7, ALU.bitwise_and, ["CM%d" % x], ["LO%d" % x], 96)
+        tt(T.HB[:, 192 * x:192 * x + 96], a, lo, ALU.subtract, ["CM%d" % x, "LO%d" % x], ["HBh%d" % x], 96, 2)
+        cp(T.HB[:, 192 * x + 96:192 * x + 192], lo, ["LO%d" % x], ["HBl%d" % x], 96)
+        dma(["K", "HBh%d" % x, "HBl%d" % x], ["K%d" % x],
+            [(T.K[2 * x + y::16, :], T.HB[:, 192 * x + 96 * y:192 * x + 96 * y + 96]) for y in (0, 1)], 2e5)
+    KK = all3("K")
+    dma(KK, ["NB"], [(T.NB[:], T.nb[:, :])], 2.5e5)
+    dma(KK, ["TR"], [(T.TR[:, :], T.tr[:, :])], 2.5e5)
+    snd("X0", ["HBh0", "HBl0"], 4.0)
+    for b in range(3):
+        snd("S0" + "abc"[b], ["S%d" % b], 6.5 + 2.0 * b)
+    for b in range(3):
+        fill(blk(T.XF, b), 0, LR, ["XF%da" % b, "XF%db" % b], True, 0.5)
+    XFK = [k + s for k in all3("XF") for s in "ab"]
+    EK = [k + s for k in all3("E") for s in "ab"]
+    dma(["LX0"], XFK, [(T.XF[y::16, :], T.LX[:, 96 * y:96 * y + 96]) for y in (0, 1)], 5e4)
+    cp(T.EXF[:, :], T.EXT[:], ["EXT"], ["EXF"], 96)
+    vec(96, 1, ["EXF"], ["EXG"], lambda q, e: q.transpose(T.EXG[:, :], T.EXF[:, :]))
+    for b in range(3):
+        cp(T.EXW[:, b::3], T.EXG[:, 32 * b:32 * b + 32], ["EXG"], ["EXW%d" % b], 32)
+    EXW = all3("EXW")
+    pool(0.37, [], ["DZ"], lambda q, e: q.iota(T.DZ[:, :], [[1, 144]], 0, -1, allow_small_or_imprecise_dtypes=True))
+    pool(0.14, [], ["PF1"], lambda q, e: q.iota(T.PF[:, 1:4], [[1, 3]], 0, 0, allow_small_or_imprecise_dtypes=True))
+    ts(T.PC[:, 2:3], T.PC[:, 1:2], 1, ALU.arith_shift_right, ["PC1"], ["PC2"], 1)
+    cp(T.PF[:, 7:8], T.PC[:, 2:3], ["PC2"], ["PF7"], 1)
+    ts(T.PF[:, 4:7], T.PF[:, 1:4], T.PF[:, 7:8], ALU.is_equal, ["PF7", "PF1"], ["PF4"], 3)
+    vec(144, 1, ["DZ", "PF0"], ["ZB"], lambda q, e: q.tensor_scalar(T.ZB[:, :], T.DZ[:, :], T.PF[:, 0:1], 15.0, ALU.add, ALU.is_equal))
+    for z in range(3):
+        ts(T.Z[:, 144 * z:144 * z + 144], T.ZB[:, :], T.PF[:, 4 + z:5 + z], ALU.mult, ["ZB", "PF4"], ["Z%d" % z], 144, 0.5)
+    ts(T.Z[:, 432:576], T.ZB[:, :], 16384.0, ALU.mult, ["ZB"], ["Z3"], 144, 0.5)
+    pool(0.4, [], ["D2"], lambda q, e: q.iota(T.D2[:, :], [[1, 160]], 128, -1))
+    ts(T.D2[:, :], T.D2[:, :], 127, ALU.bitwise_and, ["D2"], ["D2"], 160)
+    ts(T.I2[:, :], T.D2[:, :], 0.0, ALU.is_equal, ["D2"], ["I2"], 160)
+    vec(640, 0.5, [], ["ONE"], lambda q, e: q.memset(T.ONE[:, :], 1.0))
+    pool(0.17 + 1280 * CYC, ["ONE"], ["WS"], lambda q, e: q.affine_select(T.WS[:, :], T.ONE[:, :], [[-1, 5], [-5, 8], [0, 16]], ALU.is_equal, 0.0, 0, 1))
+    for (buf, key, n, vals) in ((T.D0, "D0c", LR, (0.0, None, 1.0)), (T.D0F, "D0F", LR // 2, (0.0, -1.0, 1.0))):
+        for s in range(3):
+            if vals[s] is not None:
+                fill(buf[:, s::3], vals[s], n, [key + str(s)], True)
+    cp(T.NBW[:, :], T.NB[:], ["NB"], ["NBW"], 480)
+    for k in range(5):
+        ts(T.CODE[:, :, 32 * k:32 * k + 32], T.NB[:, :, 32 * k:32 * k + 32], float((7 - k) * 2048 + (16 * 16384 if k == 4 else 0)), ALU.add,
+           ["NB"], ["CODE%d_%d" % (t, k) for t in range(R)], 96)
+
+    def gtab(src, dst, b, sk, dk, pb, tmp, tk):
+        act(LR, [sk], ["pb%d" % pb], bank(pb), blk(src, b), ACT.Square)
+        act(LR, [sk], [tk], tmp, blk(src, b), ACT.Identity, bias=-1.5)
+        tt(blk(dst, b), bank(pb), tmp, ALU.mult, ["pb%d" % pb, tk], [dk], LR)
+
+    for b in range(3):
+        gtab(T.S, T.NG, b, "S%d" % b, "NG%d" % b, b, blk(T.QG, b + 1), "QG%d" % (b + 1))
+    for b in (1, 2):
+        tmp, tk = (blk(T.QG, 4), "QG4") if b == 1 else (blk(T.M, 3), "M3")
+        act(LR, ["S%d" % b], [tk], tmp, blk(T.S, b), ACT.Square, bias=1.0, scale=-1.0)
+        act(LR, [tk], [tk], tmp, tmp, ACT.Identity, scale=0.5)
+        tt(blk(T.Q, b), bank(b), tmp, ALU.add, ["pb%d" % b, tk], ["Q%d" % b], LR)
+    for b in range(3):
+        gtab(T.SF0, T.GF0, b, "LS0" + "abc"[b], "GF0%d" % b, (3, 4, 7)[b], blk(T.M, b), "M%d" % b)
+    SFK = {0: ["LS0a", "LS0b", "LS0c"], 1: all3("SF1"), 2: all3("SF2")}
+
+    def gather(out, src, n, rd, wr, en=("V", "A")):
+        op(list(en), {"V": tv(n, PAR["g"]), "A": ta(n, PAR["g"])}, rd, wr,
+           lambda q, e: q.tensor_copy(out, src) if e == "V" else q.activation(out, src, ACT.Identity))
+
+    def spread(tab, key, b, buf, c0, rd):
+        for h in range(2):
+            gather(blk(tab, b, h * LR // 2, LR // 2), T.K[:, 0:V].indirect(buf[:, c0 + 16 * h:c0 + 16 * h + 16]), LR // 2,
+                   KK + rd, ["%s%d%s" % (key, b, "ab"[h])])
+
+    for b in range(3):
+        spread(T.E, "E", b, T.EXW, 32 * b, EXW)
+    dma(["LS0b", "LS0c"], ["SF11", "SF12"], rot(T.SF1, LR, T.SF0, LR, 2 * LR, 1), 5e5)
+    dma(["GF01", "GF02"], ["GF11", "GF12"], rot(T.GF1, LR, T.GF0, LR, 2 * LR, 1), 5e5)
+    dma(["LS0c"], ["SF22"], rot(T.SF2, 2 * LR, T.SF0, 2 * LR, LR, 2), 2.6e5)
+    dma(["GF02"], ["GF22"], rot(T.GF2, 2 * LR, T.GF0, 2 * LR, LR, 2), 2.6e5)
+
+    def wrap(gh, z, pb, n, rd, a=0):
+        def fn(q, e):
+            for r in range(16):
+                ins = q.matmul(bank(pb, a, n), T.Z[:, 144 * z + 15 - r:144 * z + 143 - r], gh(r), r == 0, r == 15)
+            return ins
+        op(["P"], {"P": 16 * 64 * PAR["pe"]}, rd + ["Z%d" % z], ["pb%d" % pb], fn, lat=0.1)
+
+    nlink = [0]
+
+    def offk(o, h, parts_):
+        if o is None:
+            return EXW
+        return ["OFF%d_%d" % (o, hh) for hh in ((0, 1) if parts_ == 1 else (h * 2 // parts_,))]
+
+    def link(tab, tkeys, buf, c0, o_in, outs):
+        x = nlink[0] % 2
+        nlink[0] += 1
+        for h in range(2):
+            a = x * LR + h * LR // 2
+            gather(T.GH[:, a:a + LR // 2], tab[:, 0:V].indirect(buf[:, c0 + 16 * h:c0 + 16 * h + 16]), LR // 2,
+                   tkeys + offk(o_in, h, 2), ["GH%d_%d" % (x, h)])
+        LH = OPT["LH"]
+        n, w = LR // LH, 32 // LH
+        for h in range(LH):
+            a = x * LR + h * n
+            gk = ["GH%d_%d" % (x, hh) for hh in ((0, 1) if LH == 1 else (h,))]
+            for (z, pb, o) in outs:
+                pb = pb if LH == 1 else 5 + h
+                wrap(lambda r, a=a: T.GH[:, a + r:a + n:16], z, pb, w, gk)
+                cp(T.OFF[:, 32 * o + h * w:32 * o + h * w + w], bank(pb, 0, w), ["pb%d" % pb], offk(o, h, LH), w)
+
+    def fetch(tab, tkeys, buf, c0, okeys, j, slot):
+        SPLIT = OPT["SPLIT"] if j > 0 else 2
+        n = LR // SPLIT
+        for h in range(SPLIT):
+            a = j * V + 3 * n * h + slot
+            out = T.D1[:, a:a + 3 * n - 2:3]
+            src = tab[:, 0:V].indirect(buf[:, c0 + h * n // 16:c0 + (h + 1) * n // 16])
+            wr = ["D%d_%d_%d" % (j, slot, hh) for hh in ((0, 1) if SPLIT == 1 else (h * 2 // SPLIT,))]
+            op(["V", "A"], {"V": tv(n, PAR["g"]), "A": ta(n, PAR["g"])}, tkeys + offk(okeys, h, SPLIT), wr,
+               lambda q, e, out=out, src=src: q.tensor_copy(out, src) if e == "V" else q.activation(out, src, ACT.Identity))
+
+    H = LR // 2
+    for t in range(R):
+        SF, GF = T["SF%d" % t], T["GF%d" % t]
+        GFK = all3("GF%d" % t)
+        if t > 0:
+            spread(T.XF, "XF", t - 1, T["LW%d" % t], 0, ["LW%d" % t])
+        tab, tk, z = (T.K, KK, 0) if t == 0 else (T.E, EK, 2)
+        link(tab, tk, T.EXW, 32 * t, None, [(z, 5, 0)])
+        link(tab, tk, T.OFF, 0, 0, [(z, 5, 1)])
+        link(T.E, EK, T.OFF, 32, 1, [(1, 5, 3), (2, 6, 2)])
+        for j in range(3):
+            link(T.XF, XFK, T.OFF, 32 * (3 + j), 3 + j, [(z, 5, 4 + j)])
+        if t == 0:
+            dma(["LX0"], XFK, [(T.XF[4 + y:112:16, :], T.LX[16:128, 96 * y:96 * y + 96]) for y in (0, 1)]
+                + [(T.XF[116 + y:117 + y, :], T.LX[0:16, 96 * y:96 * y + 96]) for y in (0, 1)], 5e4)
+        if t == 1:
+            k0, k2 = ["XF0a", "XF0b"], ["XF2a", "XF2b"]
+            dma(k0 + k2, k0 + k2, [p for y in (0, 1) for p in (
+                (T.XF[6 + y:112:16, 0:LR], T.XF[20 + y:128:16, 0:LR]), (T.XF[118 + y:119 + y, 0:LR], T.XF[4 + y:5 + y, 0:LR]),
+                (T.XF[4 + y:96:16, 2 * LR:V], T.XF[32 + y:128:16, 2 * LR:V]), (T.XF[100 + y:128:16, 2 * LR:V], T.XF[y:32:16, 2 * LR:V]))], 3e4)
+            dma(k0, k0, [(T.XF[4 + y::16, 0:LR], T.XF[6 + y::16, 0:LR]) for y in (0, 1)], 2e4)
+        fetch(GF, GFK, T.OFF, 32 * 6, 6, 0, 0)
+        for j, o in enumerate((5, 4, 3, 2, 1, 0, None)):
+            s, sk, n_, nk = (SF, SFK[t], GF, GFK) if j < 3 else (T.S, all3("S"), T.NG, all3("NG"))
+            buf, c0, ok = (T.OFF, 32 * o, o) if o is not None else (T.EXW, 32 * t, None)
+            fetch(n_, nk, buf, c0, ok, j, 1)
+            fetch(s, sk, buf, c0, ok, j, 2)
+        for j in range(7):
+            for h in range(2):
+                a = 3 * H * h
+                d0, k0 = (T.D0F[:, :], ["D0F0", "D0F1", "D0F2"]) if j == 0 else (T.D0[:, a:a + 3 * H], ["D0c0", "D0c2", "D0s%d" % h])
+                vec(3 * H, 1, k0 + ["D%d_%d_%d" % (j, s, h) for s in range(3)], ["Y%d" % h],
+                    lambda q, e, a=a, d0=d0, j=j: q.tensor_tensor_scan(T.Y[:, a:a + 3 * H], d0, T.D1[:, j * V + a:j * V + a + 3 * H], 0.0, ALU.mult, ALU.add))
+                y = T.Y[:, a + 2:a + 3 * H:3]
+                if j < 6:
+                    b = (j + 1) * V + a
+                    act(H, ["Y%d" % h], ["D0s%d" % h], T.D0[:, a + 1:a + 3 * H - 1:3], y, ACT.Square)
+                    act(H, ["Y%d" % h], ["D%d_0_%d" % (j + 1, h)], T.D1[:, b:b + 3 * H - 2:3], y, ACT.Identity, bias=1.5, scale=-1.0)
+                else:
+                    act(H, ["Y%d" % h], ["pb%d" % (6 + h)], bank(6 + h, 0, H), y, ACT.Square)
+                    act(H, ["Y%d" % h], ["HL%d" % h], T.HL[:, H * h:H * h + H], y, ACT.Identity, bias=1.5, scale=-1.0)
+        for k in range(5):
+            op(["P"], {"P": LR * PAR["pe"]}, ["WS", "TR"], ["pb%d" % k],
+               lambda q, e, k=k, t=t: q.matmul(bank(k), T.WS[:, 128 * k:128 * k + 128], blk(T.TR, t), True, True), lat=0.1)
+        St = "S%d" % t
+        op([], {}, [], [St], None, kind="j")
+        op([], {}, [], ["Q%d" % t], None, kind="j")
+        for h in range(2):
+            p, pk = bank(6 + h, 0, H), "pb%d" % (6 + h)
+            sl = blk(T.S, t, H * h, H)
+            tt(p, p, T.HL[:, H * h:H * h + H], ALU.mult, [pk, "HL%d" % h], [pk], H)
+            tt(p, p, blk(T.NG, t, H * h, H), ALU.add, [pk, "NG%d" % t], [pk], H)
+            tt(sl, p, sl, ALU.add, [pk, St], [St + "h%d" % h], H)
+        for h in range(2):
+            p, pk = bank(6 + h, 0, H), "pb%d" % (6 + h)
+            sl, sk = blk(T.S, t, H * h, H), St + "h%d" % h
+            sq, vl = T.SQ[:, H * h:H * h + H], T.VL[:, H * h:H * h + H]
+            act(H, [sk], ["VL%d" % h], vl, sl, ACT.Square, bias=1.0, scale=-1.0)
+            act(H, ["VL%d" % h], [pk], p, vl, ACT.Identity, scale=0.5)
+            op(["V", "A"], {"V": tv(H, 2), "A": ta(H)}, [sk], ["SQ%d" % h],
+               lambda q, e, sq=sq, sl=sl: q.tensor_tensor(sq, sl, sl, ALU.mult) if e == "V" else q.activation(sq, sl, ACT.Square))
+            tt(blk(T.Q, t, H * h, H), p, sq, ALU.add, [pk, "SQ%d" % h, "Q%d" % t], ["Q%dh%d" % (t, h)], H)
+        op([], {}, [St + "h0", St + "h1"], [St], None, kind="j")
+        op([], {}, ["Q%dh0" % t, "Q%dh1" % t], ["Q%d" % t], None, kind="j")
+        if t < R - 1:
+            u = t + 1
+            snd("S%d" % u, [St], 6.0)
+            LS, lk = T["LS%d" % u], "LS%d" % u
+            dma([lk], ["SF%d%d" % (u, t)], rot(T["SF%d" % u], t * LR, LS, 0, LR, u), 2.6e5)
+            if t == 0:
+                dma([lk], ["SF20"], rot(T.SF2, 0, LS, 0, LR, 2), 2.6e5)
+        dma([St], [], [(blk(T.ys, t), blk(T.S, t))], 2.6e5)
+        for k in range(5):
+            for (a, n, en) in (((0, H, ["V"]), (H, H, ["A"])) if k == 0 else ((0, LR, ["A"]),)):
+                c = 160 * t + 32 * k + a // 16
+                out, src = blk(T.QG, k, a, n), T.Q[:, 0:V].indirect(T.NBW[:, c:c + n // 16])
+                op(en, {"V": tv(n, PAR["g"]), "A": ta(n, PAR["g"])}, all3("Q") + ["NBW"], ["QG%d" % k if a == 0 else "QG0b"],
+                   lambda q, e, out=out, src=src: q.tensor_copy(out, src) if e == "V" else q.activation(out, src, ACT.Identity))
+        tt(blk(T.M, 0), bank(0), blk(T.QG, 0), ALU.mult, ["pb0", "QG0", "QG0b"], ["M0"], LR)
+        for k in range(1, 5):
+            tt(bank(k), bank(k), blk(T.QG, k), ALU.mult, ["pb%d" % k, "QG%d" % k], ["pb%d" % k], LR)
+            if k < 4:
+                tt(blk(T.M, k), bank(k), blk(T.M, k - 1), ALU.max, ["pb%d" % k, "M%d" % (k - 1)], ["M%d" % k], LR)
+        tt(bank(0), bank(4), blk(T.M, 3), ALU.max, ["pb4", "M3"], ["pb0"], LR)
+        tt(blk(T.AV, 3), blk(T.M, 3), bank(4), ALU.is_ge, ["pb4", "M3"], ["AV3"], LR)
+        for k in (2, 0, 1):
+            tt(blk(T.AV, k), blk(T.M, k), bank(0), ALU.is_ge, ["pb0", "M%d" % k], ["AV%d" % k], LR)
+        wrap(lambda r: T.AV[:, 2 * LR + r:4 * LR:16], 3, 6, 64, ["AV2", "AV3"], 0)
+        wrap(lambda r: T.AV[:, r:2 * LR:16], 3, 5, 64, ["AV0", "AV1"], 0)
+        C = T.CODE
+        ck = lambda k: "CODE%d_%d" % (t, k)
+        tt(C[:, t, 64:128], bank(6, 0, 64), C[:, t, 64:128], ALU.add, ["pb6", ck(2), ck(3)], [ck(2), ck(3)], 64)
+        tt(C[:, t, 96:160], C[:, t, 96:160], bank(6, 0, 64), ALU.subtract, ["pb6", ck(3), ck(4)], [ck(3), ck(4)], 64)
+        tt(T.MX[:, 64:96], C[:, t, 96:128], C[:, t, 128:160], ALU.max, [ck(3), ck(4)], ["MX2"], 32)
+        tt(C[:, t, 0:64], bank(5, 0, 64), C[:, t, 0:64], ALU.add, ["pb5", ck(0), ck(1)], [ck(0), ck(1)], 64)
+        tt(C[:, t, 32:96], C[:, t, 32:96], bank(5, 0, 64), ALU.subtract, ["pb5", ck(1), ck(2)], [ck(1), ck(2)], 64)
+        tt(T.MX[:, 32:64], C[:, t, 0:32], T.MX[:, 64:96], ALU.max, [ck(0), "MX2"], ["MX1"], 32)
+        tt(T.MX[:, 0:32], C[:, t, 32:64], C[:, t, 64:96], ALU.max, [ck(1), ck(2)], ["MX0"], 32)
+        tt(T.MI[:, 0:32], T.MX[:, 0:32], T.MX[:, 32:64], ALU.max, ["MX0", "MX1"], ["MI0"], 32)
+        ts(T.MI[:, 32:64], T.MI[:, 0:32], 2047, ALU.bitwise_and, ["MI0"], ["MI1"], 32)
+        if t < R - 1:
+            u = t + 1
+            cp(T.XH[:, :], T.MI[:, 32:64], ["MI1"], ["XH"], 32)
+            op(["P"], {"P": 64 * PAR["pe"]}, ["XH", "I2"], ["pb7"],
+               lambda q, e, u=u: q.matmul(bank(7, 0, 32), T.I2[:, 16 * u:16 * u + 128], T.XH[:, :], True, True), lat=0.1)
+            cp(T["RU%d" % u][:, :], bank(7, 0, 32), ["pb7"], ["RU%d" % u], 32)
+            snd("W%d" % u, ["RU%d" % u], 3.5)
+            cp(T.NW[:, :], T.MI[:, 32:64], ["MI1"], ["NW"], 32)
+            spread(T.E, "E", t, T.NW, 0, ["NW"])
+            act(LR, [St], ["pb2"], bank(2), blk(T.S, t), ACT.Identity, bias=-1.5)
+            tt(blk(T.NG, t), bank(2), T.SQ[:, :], ALU.mult, ["pb2", "SQ0", "SQ1"], ["NG%d" % t], LR)
+            gtab(T["SF%d" % u], T["GF%d" % u], t, "SF%d%d" % (u, t), "GF%d%d" % (u, t), 3, blk(T.M, 0), "M0")
+            if t == 0:
+                dma(["GF10"], ["GF20"], rot(T.GF2, 0, T.GF1, 0, LR, 1), 2.6e5)
+        cp(T.XO[:, :], T.MI[:, 32:64], ["MI1"], ["XO"], 32)
+        vec(32, 1, ["XO"], ["XT%d" % t], lambda q, e, t=t: q.transpose(T.XT[:, 32 * t:32 * t + 32], T.XO[:, :]))
+        dma(["XT%d" % t], [], [(T.yx[q::2, t * LR:t * LR + LR], T.XT[:, 32 * t + 16 * q:32 * t + 16 * q + 16]) for q in (0, 1)], 2e4)
+    return ops
+
+
+def edges(ops):
+    last, readers, deps = {}, {}, []
+    for i, o in enumerate(ops):
+        d = {}
+        for k in o["rd"]:
+            if k in last:
+                d[last[k]] = True
+            if k[:2] == "pb":
+                for j in readers.get(k, []):
+                    if ops[j]["eng"] != o["eng"] or len(o["eng"]) > 1:
+                        d.setdefault(j, False)
+        for k in o["wr"]:
+            if k in last:
+                d[last[k]] = True
+            for j in readers.get(k, []):
+                d.setdefault(j, False)
+        d.pop(i, None)
+        deps.append(d)
+        for k in o["rd"]:
+            readers.setdefault(k, []).append(i)
+        for k in o["wr"]:
+            last[k] = i
+            readers[k] = []
+    return deps
+
+
+def plan(ops, deps):
+    n, SYNC = len(ops), PAR["sy"]
+    rank = [0.0] * n
+    for i in range(n - 1, -1, -1):
+        o = ops[i]
+        rank[i] += (min(o["dur"][e] for e in o["eng"]) if o["eng"] else 0.0) + o["lat"] + 1e-6
+        for j in deps[i]:
+            rank[j] = max(rank[j], rank[i] + SYNC)
+    for i in range(n):
+        if ops[i]["x"] is True:
+            rank[i] = 1e6 - i
+    busy = {e: [] for e in "VAPGS"}
+    start, fin, eng = [0.0] * n, [0.0] * n, [None] * n
+    for i in sorted(range(n), key=lambda i: (-rank[i], i)):
+        o = ops[i]
+        ready = max([fin[j] + SYNC for j in deps[i]] + [0.0])
+        if not o["eng"]:
+            start[i], fin[i] = ready - SYNC, ready - SYNC + o["lat"]
+            continue
+        best = None
+        for e in o["eng"]:
+            s, du = ready, o["dur"][e]
+            for (a, b) in busy[e]:
+                if s + du <= a:
+                    break
+                s = max(s, b)
+            if best is None or s + du < best[0] - 1e-9:
+                best = (s + du, s, e)
+        start[i], eng[i] = best[1], best[2]
+        fin[i] = best[0] + o["lat"]
+        busy[eng[i]].append((best[1], best[0]))
+        busy[eng[i]].sort()
+    return start, fin, eng
+
+
+def place(ops, pre, post, prio, back, pen):
+    n, sy = len(ops), PAR["sy"]
+    busy = {e: [] for e in "VAPGS"}
+    start, fin, eng = [0.0] * n, [0.0] * n, [None] * n
+    left = [len(p) for p in pre]
+    todo = sorted([i for i in range(n) if not left[i]], key=lambda i: -prio[i])
+    while todo:
+        i = todo.pop()
+        o = ops[i]
+        r = 0.0
+        for j in pre[i]:
+            if fin[j] > r:
+                r = fin[j]
+        if not o["eng"]:
+            start[i], fin[i] = r, r + o["lat"]
+        else:
+            r += sy + (o["lat"] if back else 0.0)
+            best = None
+            for e in o["eng"]:
+                s, du, bz = r, o["dur"][e], busy[e]
+                lo, hi = 0, len(bz)
+                while lo < hi:
+                    m = (lo + hi) // 2
+                    if bz[m][1] <= s:
+                        lo = m + 1
+                    else:
+                        hi = m
+                while lo < len(bz) and s + du > bz[lo][0]:
+                    s = bz[lo][1]
+                    lo += 1
+                w = s + du + (pen if e == "V" else 0.0)
+                if best is None or w < best[4] - 1e-9:
+                    best = (s + du, s, e, lo, w)
+            start[i], eng[i] = best[1], best[2]
+            fin[i] = best[0] + (0.0 if back else o["lat"])
+            busy[best[2]].insert(best[3], (best[1], best[0]))
+        new = False
+        for j in post[i]:
+            left[j] -= 1
+            if not left[j]:
+                todo.append(j)
+                new = True
+        if new:
+            todo.sort(key=lambda i: -prio[i])
+    return start, fin, eng, max(fin)
+
+
+def shake(ops, dl, succ, start, rnd):
+    n = len(ops)
+    best = None
+    cur = list(start)
+    for it in range(OPT["PASS"]):
+        for i in range(n):
+            if ops[i]["x"] is True:
+                cur[i] = i - 1e6
+        pen = OPT["PEN"] * rnd(1000) / 1000.0
+        st, fin, eng, end = place(ops, dl, succ, cur, False, pen)
+        if best is None or end < best[3]:
+            best = (st, fin, eng, end)
+        if it % 4 == 3:
+            st, fin = best[0], best[1]
+        amp = OPT["AMP"] * rnd(1000) / 1000.0
+        bs, bf, be, bend = place(ops, succ, dl, [-f + amp * rnd(1000) / 1000.0 for f in fin], True, pen)
+        cur = [-f + amp * rnd(1000) / 1000.0 for f in bf]
+    for it in range(OPT["LNS"]):
+        st, fin, eng, end = best
+        a = rnd(int(end)) - 3.0
+        b = a + 3 + rnd(14)
+        amp, pen = OPT["AMP"] * rnd(1000) / 1000.0, OPT["PEN"] * rnd(1000) / 1000.0
+        loc = [dict(o, eng=o["eng"] if a <= st[i] <= b or eng[i] is None else [eng[i]]) for i, o in enumerate(ops)]
+        nz = lambda i: amp * rnd(1000) / 1000.0 if a <= st[i] <= b else amp / 2
+        if rnd(2):
+            bs, bf, be, bend = place(loc, succ, dl, [-fin[i] + nz(i) for i in range(n)], True, pen)
+            cur = [-bf[i] if a <= st[i] <= b else st[i] + end - bend - end for i in range(n)]
+            cur = [cur[i] if a <= st[i] <= b else st[i] - end for i in range(n)]
+        else:
+            cur = [st[i] + nz(i) for i in range(n)]
+        for i in range(n):
+            if ops[i]["x"] is True:
+                cur[i] = i - 1e6
+        c = place(loc, dl, succ, cur, False, pen)
+        if c[3] <= end + 1e-9:
+            best = c
+    return best
+
+
+def replay(seq, eng, dl, dur, lat, sy):
+    fin = [0.0] * len(dl)
+    start = [0.0] * len(dl)
+    free = {"V": 0.0, "A": 0.0, "P": 0.0, "G": 0.0, "S": 0.0}
+    for i in seq:
+        r = 0.0
+        for j in dl[i]:
+            if fin[j] > r:
+                r = fin[j]
+        e = eng[i]
+        if e is None:
+            start[i] = r
+            fin[i] = r + lat[i]
+        else:
+            r += sy
+            if free[e] > r:
+                r = free[e]
+            start[i] = r
+            r += dur[i][e]
+            free[e] = r
+            fin[i] = r + lat[i]
+    return max(fin), start
+
+
+def arrange(T):
+    sets = []
+    for p in PARS:
+        PAR.update(p)
+        ops = build(T)
+        sets.append(([o["dur"] for o in ops], [o["lat"] for o in ops], p["sy"]))
+    PAR.update(PARS[0])
+    ops = build(T)
+    deps = edges(ops)
+    start, fin, eng = plan(ops, deps)
+    n = len(ops)
+    dl = [list(d) for d in deps]
+    succ = [[] for o in ops]
+    for i in range(n):
+        for j in dl[i]:
+            succ[j].append(i)
+    x = [OPT["SEED"]]
+
+    def rnd(m):
+        x[0] = (x[0] * 6364136223846793005 + 1442695040888963407) % (1 << 64)
+        return (x[0] >> 33) % m
+
+    start, fin, eng, end = shake(ops, dl, succ, start, rnd)
+    seq = sorted(range(n), key=lambda i: (start[i], i))
+    base = [replay(seq, eng, dl, *s)[0] for s in sets]
+
+    def score(sq, en):
+        return sum(replay(sq, en, dl, *s)[0] / b for s, b in zip(sets, base))
+
+    best = score(seq, eng)
+    first = [i for i in range(n) if ops[i]["x"] is True]
+    mov = [i for i in range(n) if eng[i] is not None and i not in first]
+    for step in range(OPT["STEPS"]):
+        i = mov[rnd(len(mov))]
+        en = eng
+        if len(ops[i]["eng"]) > 1 and rnd(2) == 0:
+            en = list(eng)
+            en[i] = [e for e in ops[i]["eng"] if e != eng[i]][0]
+        p = seq.index(i)
+        sq = seq[:p] + seq[p + 1:]
+        k = rnd(3) + (0 if en is not eng else 1)
+        if rnd(2):
+            q, stop = p, set(dl[i] + first)
+            while q > 0 and k > 0 and sq[q - 1] not in stop:
+                q -= 1
+                k -= en[sq[q]] == en[i]
+        else:
+            q, stop = p, set(succ[i])
+            while q < n - 1 and k > 0 and sq[q] not in stop:
+                k -= en[sq[q]] == en[i]
+                q += 1
+        if q == p and en is eng:
+            continue
+        sq.insert(q, i)
+        s = score(sq, en)
+        if s <= best:
+            best, seq, eng = s, sq, en
+            if step % 8 == 0:
+                st = replay(seq, eng, dl, *sets[0])[1]
+                pos = {j: a for a, j in enumerate(seq)}
+                seq = sorted(seq, key=lambda j: (st[j], pos[j]))
+    return deps, seq, eng, [replay(seq, eng, dl, *s)[0] for s in sets], base
+
+
+PLAN = {}
+
+
+def rank_program(g, core, T, topo):
+    rank = T.rank_of(core)
+    if rank is None:
+        helper_program(g, core, T, topo)
+        return
+    n = len(T.cores)
+    dst, src = T.cores[(rank - 1) % n], T.cores[(rank + 1) % n]
+    if not PLAN:
+        PLAN["plan"] = arrange(T)
+    ops = build(T)
+    deps, seq, eng = PLAN["plan"][:3]
+    Qs = {"V": g.vector, "A": g.scalar, "P": g.tensor, "G": g, "S": g.sync}
+    clock = {e: {} for e in Qs}
+    count = {}
+    tok = {}
+    ndma = [0]
+    for i in seq:
+        o, e = ops[i], eng[i]
+        if o["kind"] == "a":
+            m = o["x"]
+            c = arrivals(T, topo, src, core, message(T, m)[5])
+            count["a" + m] = c
+            tok[i] = [("a" + m, c, {}, None)]
+            continue
+        if o["kind"] == "j":
+            top = {}
+            for j in deps[i]:
+                for x in tok[j]:
+                    if x[0] not in top or top[x[0]][1] < x[1]:
+                        top[x[0]] = x
+            tok[i] = list(top.values())
+            continue
+        need = {}
+        for j, hard in deps[i].items():
+            if o["kind"] == "s" and ops[j]["kind"] == "s":
+                continue
+            for x in tok[j]:
+                if x[3] == e and not hard:
+                    continue
+                if x[0] not in need or need[x[0]][1] < x[1]:
+                    need[x[0]] = x
+        ck = clock[e]
+        todo = sorted(need.values(), key=lambda x: -len(x[2]))
+        for (s, c, known, qq) in todo:
+            if ck.get(s, 0) < c:
+                Qs[e].wait_ge(T.sem[s], c)
+                ck[s] = c
+                for s2, c2 in known.items():
+                    if ck.get(s2, 0) < c2:
+                        ck[s2] = c2
+        if o["kind"] == "c":
+            s = "c" + e
+            o["fn"](Qs[e], e).then_inc(T.sem[s], 1)
+            count[s] = count.get(s, 0) + 1
+            tok[i] = [(s, count[s], dict(ck), e)]
+        elif o["kind"] == "d":
+            s = "d%d" % ndma[0]
+            ndma[0] += 1
+            for (a, b) in o["fn"]:
+                Qs[e].dma_start(a, b).then_inc(T.sem[s], 16)
+            count[s] = 16 * len(o["fn"])
+            tok[i] = [(s, count[s], dict(ck), None)]
+        else:
+            s = "l" + o["x"]
+            count[s] = send(g, T, topo, core, dst, o["x"])
+            tok[i] = [(s, count[s], dict(ck), None)]
+    for s, c in count.items():
+        if clock["G"].get(s, 0) < c:
+            g.wait_ge(T.sem[s], c)

@@ -2,49 +2,47 @@ from concourse.bass import DstId, RemoteDMATransfer
 from concourse.mybir import AluOpType as ALU, ActivationFunctionType as ACT
 
 V, LR, R = 1536, 512, 3
-F32, I32, U16, F16, BF = "float32", "int32", "uint16", "float16", "bfloat16"
+H = LR // 2
+F32, I32, U16, BF = "float32", "int32", "uint16", "bfloat16"
 SCRATCH = {
-    "S": ("sbuf", [128, V], F32), "NG": ("sbuf", [128, V], F32), "Q": ("sbuf", [128, V], F32),
+    "S": ("sbuf", [128, V], F32), "NG": ("sbuf", [128, V], F32), "Q": ("sbuf", [128, 2 * V], F32), "SQ": ("sbuf", [128, 2 * V], F32),
     "SF0": ("sbuf", [128, V], F32), "SF1": ("sbuf", [128, V], F32), "SF2": ("sbuf", [128, V], F32),
     "GF0": ("sbuf", [128, V], F32), "GF1": ("sbuf", [128, V], F32), "GF2": ("sbuf", [128, V], F32),
     "K": ("sbuf", [128, V], BF), "E": ("sbuf", [128, V], BF), "XF": ("sbuf", [128, V], BF),
-    "CM": ("sbuf", [128, 288], I32), "LO": ("sbuf", [128, 288], I32), "HB": ("sbuf", [128, 576], BF),
-    "D1": ("sbuf", [128, 7 * V], F32), "D0": ("sbuf", [128, V], F32), "D0F": ("sbuf", [128, V // 2], F32),
-    "Y": ("sbuf", [128, V], F32),
-    "LS1": ("sbuf", [128, LR], F32), "LS2": ("sbuf", [128, LR], F32),
-    "LW1": ("sbuf", [128, 32], U16), "LW2": ("sbuf", [128, 32], U16), "LX": ("sbuf", [128, 192], BF),
+    "CM": ("sbuf", [128, 96], I32), "CW": ("sbuf", [128, 384], I32), "HB": ("sbuf", [128, 768], BF),
+    "D1": ("sbuf", [128, 8 * V], F32), "D0": ("sbuf", [128, V], F32), "Y": ("sbuf", [128, V], F32), "DQ": ("sbuf", [128, LR], F32),
+    "LS1": ("sbuf", [128, LR], F32), "LS2": ("sbuf", [128, LR], F32), "LG": ("sbuf", [128, LR], F32), "TF": ("sbuf", [128, V], F32),
+    "LW1": ("sbuf", [128, 32], U16), "LW2": ("sbuf", [128, 32], U16), "LX": ("sbuf", [128, 192], BF), "LI": ("sbuf", [128, 96], I32),
     "QG": ("sbuf", [128, 5 * LR], F32), "M": ("sbuf", [128, 4 * LR], F32), "AV": ("sbuf", [128, 4 * LR], BF),
-    "HL": ("sbuf", [128, LR], F32), "VL": ("sbuf", [128, LR], F32), "SQ": ("sbuf", [128, LR], F32),
-    "GH": ("sbuf", [128, 2 * LR], BF), "OFF": ("sbuf", [128, 7 * 32], U16),
-    "EXT": ("sbuf", [128, 3, 32], I32), "EXF": ("sbuf", [128, 96], F32),
-    "EXG": ("sbuf", [128, 96], F32), "EXW": ("sbuf", [128, 96], U16),
-    "NB": ("sbuf", [128, 3, 160], I32), "NBW": ("sbuf", [128, 480], U16), "CODE": ("sbuf", [128, 3, 160], F32),
+    "GH": ("sbuf", [128, 2 * LR], BF), "OFF": ("sbuf", [128, 7 * 32], U16), "EXW": ("sbuf", [128, 96], U16),
+    "NIL": ("sbuf", [128, LR], BF), "CK": ("sbuf", [1, 128], BF), "W0": ("sbuf", [128, V], BF),
+    "NB": ("sbuf", [128, 3, 160], I32), "NBW": ("sbuf", [128, 480], U16), "CODE": ("sbuf", [128, 18, 32], F32),
     "TR": ("sbuf", [40, V], BF), "ONE": ("sbuf", [40, 640], BF), "WS": ("sbuf", [40, 640], BF),
     "DZ": ("sbuf", [128, 144], F32), "PC": ("sbuf", [128, 4], I32), "PF": ("sbuf", [128, 12], F32),
     "ZB": ("sbuf", [128, 144], BF), "Z": ("sbuf", [128, 4 * 144], BF),
-    "D2": ("sbuf", [128, 160], I32), "I2": ("sbuf", [128, 160], F16),
-    "MX": ("sbuf", [128, 96], F32), "MI": ("sbuf", [128, 64], I32), "NW": ("sbuf", [128, 32], U16),
-    "XH": ("sbuf", [128, 32], F16), "RU1": ("sbuf", [128, 32], U16), "RU2": ("sbuf", [128, 32], U16),
+    "D2": ("sbuf", [128, 160], I32), "I2": ("sbuf", [128, 160], F32),
+    "MX": ("sbuf", [128, 64], F32), "MI": ("sbuf", [128, 64], I32), "NW": ("sbuf", [128, 32], U16),
+    "RU1": ("sbuf", [128, 32], U16), "RU2": ("sbuf", [128, 32], U16),
     "XO": ("sbuf", [128, 32], F32), "XT": ("sbuf", [128, 96], F32),
     "PS": ("psum", [128, 8 * LR], F32),
 }
-MSGS = ["X0", "S0a", "S0b", "S0c", "S1", "W1", "S2", "W2"]
+MSGS = ["X0"] + ["S0%d" % p for p in range(6)] + ["G00", "G01", "S1", "W1", "S2", "W2"]
 NDMA = 40
 SEMAPHORES = ["cV", "cA", "cP", "cG"] + ["a" + m for m in MSGS] + ["l" + m for m in MSGS] + ["d%d" % i for i in range(NDMA)]
+CHAINS = [(0, 192), (192, 160), (352, 160)]
 
 CYC = 0.83e-3
 PARS = [
-    {"f": 1.25, "g": 1.55, "pe": 0.6e-3, "sy": 0.06, "dl": 2.0, "rl": 1.0, "add": 1},
-    {"f": 1.1, "g": 1.95, "pe": 0.5e-3, "sy": 0.1, "dl": 1.5, "rl": 1.3, "add": 1},
-    {"f": 1.35, "g": 1.15, "pe": 1.0e-3, "sy": 0.04, "dl": 2.3, "rl": 0.8, "add": 0},
+    {"f": 1.05, "g": 1.56, "pe": 0.5e-3, "sy": 0.11, "dl": 1.6, "bw": 4e5, "rl": 0.65},
+    {"f": 1.35, "g": 1.95, "pe": 0.57e-3, "sy": 0.08, "dl": 1.7, "bw": 3e5, "rl": 0.75},
+    {"f": 1.0, "g": 1.2, "pe": 0.5e-3, "sy": 0.15, "dl": 1.8, "bw": 3e5, "rl": 0.75},
 ]
 PAR = dict(PARS[0])
-OPT = {"LH": 1, "SPLIT": 2, "STEPS": 5000, "SEED": 5, "PASS": 100, "AMP": 1.2, "PEN": 1.5, "LNS": 4500}
+OPT = {"TRIES": 24000, "SEED": 5, "WIN": 110, "HEAT": 0.008, "BACK": 0.8, "AMP": 1.2, "PEN": 1.5, "PULL": 0.01, "WEIGHT": [2, 1, 1]}
 
 
 def tv(n, c=1.0, f0=0.055):
-    x = n * c * CYC
-    return PAR["f"] * (f0 + x if PAR["add"] or c == PAR["g"] else max(f0, x))
+    return PAR["f"] * (f0 + n * c * CYC)
 
 
 def ta(n, c=1.0):
@@ -53,87 +51,70 @@ def ta(n, c=1.0):
 
 def message(T, m):
     if m == "X0":
-        return T.HB, 0, T.LX, 0, 192, False
+        return T.CM, 0, T.LI, 0, 96
     if m[0] == "W":
-        return T["RU" + m[1]], 0, T["LW" + m[1]], 0, 32, False
+        return T["RU" + m[1]], 0, T["LW" + m[1]], 0, 32
     if m[1] == "0":
-        b = "abc".index(m[2])
-        return T.S, b * LR, T.SF0, b * LR, LR, True
-    return T.S, (int(m[1]) - 1) * LR, T["LS" + m[1]], 0, LR, True
+        c = int(m[2]) * H
+        return (T.S, c, T.SF0, c, H) if m[0] == "S" else (T.NG, c, T.GF0, c, H)
+    return T.S, (int(m[1]) - 1) * LR, T["LS" + m[1]], 0, LR
 
 
 def bits(mask):
     return bin(mask).count("1")
 
 
-def helpers(T, topo, src, dst):
-    hs = [c for c in topo.cores_of(src) if T.rank_of(c) is None and topo.may_write(c, dst)]
-    return sorted(hs, key=lambda c: (topo.die(c) != topo.die(src), c))
-
-
-def parts(topo, src, h, n):
-    es = topo.engines(src, h)
-    k = len(es) // n
-    return [sum(1 << e for e in es[i * k:(i + 1) * k]) for i in range(n)]
-
-
-def arrivals(T, topo, src, dst, wide):
+def legs(T, topo, src, dst, m):
     if topo.may_write(src, dst):
-        return bits(topo.mask(src, dst))
-    hs = helpers(T, topo, src, dst)
-    return sum(bits(topo.mask(h, dst)) for h in (hs if wide else hs[:1]))
+        return [(dst, topo.mask(src, dst))]
+    near = [c for c in topo.cores_of(src) if T.rank_of(c) is None and topo.may_write(c, dst)]
+    near = [c for c in near if all(topo.die(x) != topo.die(c) for x in near if x < c)]
+    near.sort(key=lambda c: topo.die(c) != topo.die(src))
+    if m[0] == "W" or len(m) == 3:
+        c = near[int(m[2]) % len(near) if len(m) == 3 else 0]
+        return [(c, topo.mask(src, c))]
+    es = topo.engines(src, near[0])
+    k = len(es) // len(near)
+    return [(c, sum(1 << e for e in es[i * k:(i + 1) * k])) for i, c in enumerate(near)]
+
+
+def arrivals(T, topo, src, dst, m):
+    return sum(bits(mask if c == dst else topo.mask(c, dst)) for c, mask in legs(T, topo, src, dst, m))
 
 
 def send(g, T, topo, src, dst, m):
-    sb, so, lb, lo, n, wide = message(T, m)
-    if topo.may_write(src, dst):
-        rid, pid = topo.addr(dst, src)
-        g.remote_dma(lb[:, lo:lo + n], sb[:, so:so + n], T.sem["a" + m], T.sem["l" + m], pid, rid, topo.mask(src, dst))
-        return bits(topo.mask(src, dst))
-    hs = helpers(T, topo, src, dst)
-    if not wide:
-        rid, pid = topo.addr(hs[0], src)
-        g.remote_dma(lb[:, lo:lo + n], sb[:, so:so + n], T.sem["a" + m], T.sem["l" + m], pid, rid, topo.mask(src, hs[0]))
-        return bits(topo.mask(src, hs[0]))
-    w = n // len(hs)
-    ms = parts(topo, src, hs[0], len(hs))
-    trs = []
-    for i, h in enumerate(hs):
-        rid, pid = topo.addr(h, src)
-        trs.append(RemoteDMATransfer(dst_ids=[DstId(rid=rid, pnc=pid)], dma_engine_mask=ms[i], remote_sem=T.sem["a" + m],
-                                     src=sb[:, so + i * w:so + (i + 1) * w], dst=lb[:, lo + i * w:lo + (i + 1) * w]))
-    g.remote_dma_fused(trs, local_sem=T.sem["l" + m])
-    return sum(bits(x) for x in ms)
+    sb, so, lb, lo, n = message(T, m)
+    ls = legs(T, topo, src, dst, m)
+    w = n // len(ls)
+    sides = [(lb[:, lo + i * w:lo + (i + 1) * w], sb[:, so + i * w:so + (i + 1) * w]) for i in range(len(ls))]
+    if len(ls) == 1:
+        rid, pid = topo.addr(ls[0][0], src)
+        g.remote_dma(sides[0][0], sides[0][1], T.sem["a" + m], T.sem["l" + m], pid, rid, ls[0][1])
+    else:
+        g.remote_dma_fused([RemoteDMATransfer(dst_ids=[DstId(rid=topo.addr(c, src)[0], pnc=topo.addr(c, src)[1])], dma_engine_mask=mask,
+                                              remote_sem=T.sem["a" + m], src=s, dst=o) for (c, mask), (o, s) in zip(ls, sides)],
+                           local_sem=T.sem["l" + m])
+    return sum(bits(mask) for c, mask in ls)
 
 
-def helper_program(g, core, T, topo):
+def relay_program(g, core, T, topo):
     n = len(T.cores)
-    for r in range(n):
-        src, dst = T.cores[r], T.cores[(r - 1) % n]
-        if topo.may_write(src, dst):
-            continue
-        hs = helpers(T, topo, src, dst)
-        if core not in hs:
-            continue
-        i = hs.index(core)
-        rid, pid = topo.addr(dst, core)
-        mask = topo.mask(core, dst)
-        sent = []
-        for m in MSGS:
-            sb, so, lb, lo, w, wide = message(T, m)
-            if wide:
-                w = w // len(hs)
-                lo = lo + i * w
-                got = bits(parts(topo, src, hs[0], len(hs))[i])
-            elif i == 0:
-                got = bits(topo.mask(src, core))
-            else:
-                continue
-            g.wait_ge(T.sem["a" + m], got)
-            g.remote_dma(lb[:, lo:lo + w], lb[:, lo:lo + w], T.sem["a" + m], T.sem["l" + m], pid, rid, mask)
-            sent.append(m)
-        for m in sent:
-            g.wait_ge(T.sem["l" + m], bits(mask))
+    sent = []
+    for m in MSGS:
+        for r in range(n):
+            src, dst = T.cores[r], T.cores[(r - 1) % n]
+            ls = legs(T, topo, src, dst, m)
+            for i, (c, got) in enumerate(ls):
+                if c == core:
+                    sb, so, lb, lo, w = message(T, m)
+                    w //= len(ls)
+                    piece = lb[:, lo + i * w:lo + (i + 1) * w]
+                    rid, pid = topo.addr(dst, core)
+                    g.wait_ge(T.sem["a" + m], bits(got))
+                    g.remote_dma(piece, piece, T.sem["a" + m], T.sem["l" + m], pid, rid, topo.mask(core, dst))
+                    sent.append((m, bits(topo.mask(core, dst))))
+    for m, c in sent:
+        g.wait_ge(T.sem["l" + m], c)
 
 
 def build(T):
@@ -141,6 +122,9 @@ def build(T):
 
     def op(eng, dur, rd, wr, fn, lat=0.0, kind="c", extra=None):
         ops.append({"eng": eng, "dur": dur, "rd": rd, "wr": wr, "fn": fn, "lat": lat, "kind": kind, "x": extra})
+
+    def join(rd, wr, lat=0.0):
+        op([], {}, rd, wr, None, lat=lat, kind="j")
 
     def vec(n, c, rd, wr, fn):
         op(["V"], {"V": tv(n, c)}, rd, wr, fn)
@@ -156,27 +140,36 @@ def build(T):
         op(["A", "V"] if both else ["A"], {"A": ta(n), "V": tv(n, 2 if func == ACT.Square else 1)}, rd, wr, fn)
 
     def dma(rd, wr, pairs, nbytes, eng="S", first=False):
-        op([eng], {eng: 0.1 * len(pairs)}, rd, wr, pairs, lat=PAR["dl"] + nbytes / 2.5e5, kind="d", extra=first)
+        op([eng], {eng: 0.1 * len(pairs)}, rd, wr, pairs, lat=PAR["dl"] + nbytes / PAR["bw"], kind="d", extra=first)
 
     def pool(dur, rd, wr, fn):
         op(["G"], {"G": dur * PAR["f"]}, rd, wr, fn)
 
-    def fill(ap, x, n, wr, fl, c=1.0):
-        def fn(q, e):
-            if e == "V":
-                return q.memset(ap, float(x))
-            return q.iota(ap, [[0, n]], int(x), 0, allow_small_or_imprecise_dtypes=True)
-        op(["V", "G"], {"V": tv(n, c), "G": PAR["f"] * (0.13 + 2 * n * CYC)}, [], wr, fn)
+    def fill(ap, pattern, base, n, wr):
+        pool(0.13 + 2 * n * CYC, ["sentS05"], wr, lambda q, e: q.iota(ap, pattern, base, 0, allow_small_or_imprecise_dtypes=True))
 
-    def snd(m, rd, lat):
-        op(["G"], {"G": 2.3 if m == "X0" else 0.3}, rd, ["sent" + m, "order"], None, lat=0.0, kind="s", extra=m)
-        op([], {}, ["sent" + m], ["L" + m], None, lat=(1.5 + lat) * PAR["rl"], kind="a", extra=m)
+    def clear(ap, wr):
+        op(["A"], {"A": ta(LR)}, ["NIL"], wr, lambda q, e: q.activation(ap, T.NIL[:, :], ACT.Identity))
 
-    def bank(b, a=0, n=LR):
-        return T.PS[:, b * LR + a:b * LR + a + n]
+    def pe(cycles, rd, pb, fn):
+        op(["P"], {"P": cycles * PAR["pe"]}, rd, ["pb%d" % pb], fn, lat=0.1)
+
+    def snd(m, rd, left, landed):
+        op(["G"], {"G": 2.3 if m == "X0" else 0.3}, rd, ["sent" + m, "order"], None, kind="s", extra=m)
+        op([], {}, ["sent" + m], ["L" + m], None, lat=landed * PAR["rl"], kind="a", extra=m)
+        join(["sent" + m], ["left" + m], left * PAR["rl"])
+
+    def bank(b, n=LR):
+        return T.PS[:, b * LR:b * LR + n]
 
     def blk(t, b, a=0, n=LR):
         return t[:, b * LR + a:b * LR + a + n]
+
+    def pair(buf, b, a, n, s):
+        return buf[:, 2 * (b * LR + a) + s:2 * (b * LR + a + n) - 1 + s:2]
+
+    def slot(buf, j, s, a, n):
+        return buf[:, j * V + 3 * a + s:j * V + 3 * (a + n) - 2 + s:3]
 
     def tt(out, a, b, o, rd, wr, n, c=1.0):
         vec(n, c, rd, wr, lambda q, e: q.tensor_tensor(out, a, b, o))
@@ -184,8 +177,18 @@ def build(T):
     def ts(out, a, s, o, rd, wr, n, c=1.0):
         vec(n, c, rd, wr, lambda q, e: q.tensor_scalar(out, a, s, None, o))
 
-    def cp(out, a, rd, wr, n, c=1.0):
-        vec(n, c, rd, wr, lambda q, e: q.tensor_copy(out, a))
+    def cp(out, a, rd, wr, n):
+        vec(n, 1, rd, wr, lambda q, e: q.tensor_copy(out, a))
+
+    def scan(out, d0, d1, rd, wr, n):
+        vec(n, 1, rd, wr, lambda q, e: q.tensor_tensor_scan(out, d0, d1, 0.0, ALU.mult, ALU.add))
+
+    def gather(out, src, n, rd, wr):
+        op(["V", "A"], {"V": tv(n, PAR["g"]), "A": ta(n, PAR["g"])}, rd, wr,
+           lambda q, e: q.tensor_copy(out, src) if e == "V" else q.activation(out, src, ACT.Identity))
+
+    def by(tab, buf, c0, a, n):
+        return tab[:, :].indirect(buf[:, c0 + a // 16:c0 + (a + n) // 16])
 
     def rot(dst, dc, src, sc, n, t):
         s = 16 * t
@@ -194,41 +197,53 @@ def build(T):
     def all3(k):
         return [k + "0", k + "1", k + "2"]
 
-    dma([], ["CM0"], [(T.CM[:, 0:96], T.ex[:, :])], 5e4, eng="A", first=True)
-    dma([], ["EXT"], [(T.EXT[:, :, 16 * q:16 * q + 16], T.ex[q::2, :]) for q in (0, 1)], 1e5, first=True)
-    dma([], ["CM1"], [(T.CM[:, 96:192], T.pt[:, :])], 1e5, eng="A", first=True)
-    for b in range(3):
-        dma([], ["S%d" % b], [(blk(T.S, b), blk(T.sat, b))], 2.6e5 * (b + 1), eng="ASS"[b], first=True)
-    pool(0.13 + 192 * CYC, [], ["CM2"], lambda q, e: q.iota(T.CM[:, 192:288], [[1, 96]], 0, 0))
+    def un(name, a=0, n=LR):
+        return ["%s.%d" % (name, u) for u in range(a // 32, (a + n) // 32)]
+
+    def split(a, hi, lo, n, keys, out):
+        cp(hi, a, keys, [out + "h"], n)
+        tt(lo, a, hi, ALU.subtract, keys + [out + "h"], [out + "l"], n, 2)
+
+    WHOLE, HALVES = [(0, LR)], [(0, H), (H, H)]
+    FUSED = max(2, PAR["g"])
+    dma([], ["CM0"], [(T.CM[:, :], T.ex[:, :])], 5e4, eng="A", first=True)
+    dma([], ["CW0"], [(T.CW[0:64, 0:192], T.ex[:, :])], 1e5, first=True)
+    dma([], ["CW1"], [(T.CW[64:128, 0:192], T.pt[:, :])], 1e5, eng="A", first=True)
+    for b in range(2):
+        dma([], ["S%d" % b], [(blk(T.S, b), blk(T.sat, b))], 2.6e5 * (b + 1.5), first=True)
+    pool(0.13 + 384 * CYC, [], ["CW2"], lambda q, e: q.iota(T.CW[0:64, 192:384], [[1, 192]], 0, 0))
     pool(0.14, [], ["PC0"], lambda q, e: q.iota(T.PC[:, 0:1], [[1, 1]], 0, 1))
     ts(T.PC[:, 1:2], T.PC[:, 0:1], 15, ALU.bitwise_and, ["PC0"], ["PC1"], 1)
     cp(T.PF[:, 0:1], T.PC[:, 1:2], ["PC1"], ["PF0"], 1)
-    ts(T.PF[:, 8:9], T.PC[:, 1:2], 96.0, ALU.mult, ["PC1"], ["PF8"], 1)
-    ts(T.CM[:, 192:288], T.CM[:, 192:288], T.PF[:, 8:9], ALU.add, ["CM2", "PF8"], ["CM2"], 96)
-    vec(V, 0.5, [], ["K"], lambda q, e: q.memset(T.K[:, :], 0.0))
-    for x in range(3):
-        a, lo = T.CM[:, 96 * x:96 * x + 96], T.LO[:, 96 * x:96 * x + 96]
-        ts(lo, a, 7, ALU.bitwise_and, ["CM%d" % x], ["LO%d" % x], 96)
-        tt(T.HB[:, 192 * x:192 * x + 96], a, lo, ALU.subtract, ["CM%d" % x, "LO%d" % x], ["HBh%d" % x], 96, 2)
-        cp(T.HB[:, 192 * x + 96:192 * x + 192], lo, ["LO%d" % x], ["HBl%d" % x], 96)
-        dma(["K", "HBh%d" % x, "HBl%d" % x], ["K%d" % x],
-            [(T.K[2 * x + y::16, :], T.HB[:, 192 * x + 96 * y:192 * x + 96 * y + 96]) for y in (0, 1)], 2e5)
+    ts(T.PC[:, 3:4], T.PC[:, 0:1], 7, ALU.bitwise_and, ["PC0"], ["PC3"], 1)
+    ts(T.PF[:, 8:9], T.PC[:, 3:4], 192.0, ALU.mult, ["PC3"], ["PF8"], 1)
+    ts(T.CW[0:64, 192:384], T.CW[0:64, 192:384], T.PF[0:64, 8:9], ALU.add, ["CW2", "PF8"], ["CW2"], 192)
+    op(["V"], {"V": tv(LR, 0.5)}, [], ["NIL"], lambda q, e: q.memset(T.NIL[:, :], 0.0), extra=True)
+    for b in range(3):
+        clear(blk(T.K, b), ["Kz%d" % b])
+    join(all3("Kz"), ["K"])
+    split(T.CW[0:64, 192:384], T.HB[0:64, 384:576], T.HB[0:64, 576:768], 192, ["CW2"], "HI")
+    dma(["K", "HIh", "HIl"], ["K2"], [(T.K[4 + y::16, :], T.HB[0:64, 384 + 192 * y:576 + 192 * y]) for y in (0, 1)], 1e5)
+    split(T.CW[:, 0:192], T.HB[:, 0:192], T.HB[:, 192:384], 192, ["CW0", "CW1", "HIl"], "HB")
+    for x in range(2):
+        dma(["K", "HBh", "HBl"], ["K%d" % x],
+            [(T.K[2 * x + y::16, :], T.HB[64 * x:64 * x + 64, 192 * y:192 * y + 192]) for y in (0, 1)], 3e5)
     KK = all3("K")
-    dma(KK, ["NB"], [(T.NB[:], T.nb[:, :])], 2.5e5)
-    dma(KK, ["TR"], [(T.TR[:, :], T.tr[:, :])], 2.5e5)
-    snd("X0", ["HBh0", "HBl0"], 4.0)
+    snd("X0", ["CM0"], 1.2, 6.0)
+    join(["HBl"], ["late"], 0.6)
+    dma(["late"], ["S2"], [(blk(T.S, 2), blk(T.sat, 2))], 5.2e5)
+    for p, landed in enumerate((8, 8.5, 9, 9.5, 8.5, 9)):
+        snd("S0%d" % p, ["S%d" % (p // 2)], 2.0, landed)
     for b in range(3):
-        snd("S0" + "abc"[b], ["S%d" % b], 6.5 + 2.0 * b)
-    for b in range(3):
-        fill(blk(T.XF, b), 0, LR, ["XF%da" % b, "XF%db" % b], True, 0.5)
+        join(["LS0%d" % (2 * b), "LS0%d" % (2 * b + 1)], ["SF0%d" % b])
+        clear(blk(T.XF, b), ["XF%da" % b, "XF%db" % b])
     XFK = [k + s for k in all3("XF") for s in "ab"]
     EK = [k + s for k in all3("E") for s in "ab"]
-    dma(["LX0"], XFK, [(T.XF[y::16, :], T.LX[:, 96 * y:96 * y + 96]) for y in (0, 1)], 5e4)
-    cp(T.EXF[:, :], T.EXT[:], ["EXT"], ["EXF"], 96)
-    vec(96, 1, ["EXF"], ["EXG"], lambda q, e: q.transpose(T.EXG[:, :], T.EXF[:, :]))
-    for b in range(3):
-        cp(T.EXW[:, b::3], T.EXG[:, 32 * b:32 * b + 32], ["EXG"], ["EXW%d" % b], 32)
-    EXW = all3("EXW")
+    split(T.LI[:, :], T.LX[:, 0:96], T.LX[:, 96:192], 96, ["LX0"], "LX")
+    dma(["LXh", "LXl"], XFK, [(T.XF[y::16, :], T.LX[:, 96 * y:96 * y + 96]) for y in (0, 1)], 3e5)
+    dma(XFK, ["NB"], [(T.NB[:], T.nb[:, :])], 8e5)
+    dma(XFK, ["TR"], [(T.TR[:, :], T.tr[:, :])], 8e5)
+    dma(["TR"], ["W0"], [(T.W0[p::16, :], T.tr[0::5, :]) for p in range(16)], 8e5)
     pool(0.37, [], ["DZ"], lambda q, e: q.iota(T.DZ[:, :], [[1, 144]], 0, -1, allow_small_or_imprecise_dtypes=True))
     pool(0.14, [], ["PF1"], lambda q, e: q.iota(T.PF[:, 1:4], [[1, 3]], 0, 0, allow_small_or_imprecise_dtypes=True))
     ts(T.PC[:, 2:3], T.PC[:, 1:2], 1, ALU.arith_shift_right, ["PC1"], ["PC2"], 1)
@@ -241,105 +256,98 @@ def build(T):
     pool(0.4, [], ["D2"], lambda q, e: q.iota(T.D2[:, :], [[1, 160]], 128, -1))
     ts(T.D2[:, :], T.D2[:, :], 127, ALU.bitwise_and, ["D2"], ["D2"], 160)
     ts(T.I2[:, :], T.D2[:, :], 0.0, ALU.is_equal, ["D2"], ["I2"], 160)
-    vec(640, 0.5, [], ["ONE"], lambda q, e: q.memset(T.ONE[:, :], 1.0))
+    fill(T.ONE[:, :], [[0, 640]], 1, 640, ["ONE"])
     pool(0.17 + 1280 * CYC, ["ONE"], ["WS"], lambda q, e: q.affine_select(T.WS[:, :], T.ONE[:, :], [[-1, 5], [-5, 8], [0, 16]], ALU.is_equal, 0.0, 0, 1))
-    for (buf, key, n, vals) in ((T.D0, "D0c", LR, (0.0, None, 1.0)), (T.D0F, "D0F", LR // 2, (0.0, -1.0, 1.0))):
-        for s in range(3):
-            if vals[s] is not None:
-                fill(buf[:, s::3], vals[s], n, [key + str(s)], True)
-    cp(T.NBW[:, :], T.NB[:], ["NB"], ["NBW"], 480)
-    for k in range(5):
-        ts(T.CODE[:, :, 32 * k:32 * k + 32], T.NB[:, :, 32 * k:32 * k + 32], float((7 - k) * 2048 + (16 * 16384 if k == 4 else 0)), ALU.add,
-           ["NB"], ["CODE%d_%d" % (t, k) for t in range(R)], 96)
+    fill(T.D0[:, 0::3], [[0, LR]], 0, LR, ["D0c0"])
+    fill(T.D0[:, 2::3], [[0, LR]], 1, LR, ["D0c2"])
+    fill(T.DQ[:, :], [[0, H], [2, 2]], 0, LR, ["DQ"])
+    for t in range(R):
+        vec(160, 1, ["NB"], ["NBW%d" % t], lambda q, e, t=t: q.tensor_scalar(T.NBW[:, 160 * t:160 * t + 160], T.NB[:, t, :], 2.0, 1.0, ALU.mult, ALU.add))
+    for c, (base, step) in enumerate(((7, 6), (18, 4))):
+        fill(T.CK[:, 64 * c:64 * c + 64], [[step * 2048, 2], [0, 32]], base * 2048, 64, ["CK%d" % c])
+    ts(T.CODE[:, 5::6, :], T.NB[:, :, 128:160], float(25 * 2048 + 16 * 16384), ALU.add, ["NB"], ["CODE%d_5" % t for t in range(R)], 96)
 
-    def gtab(src, dst, b, sk, dk, pb, tmp, tk):
-        act(LR, [sk], ["pb%d" % pb], bank(pb), blk(src, b), ACT.Square)
-        act(LR, [sk], [tk], tmp, blk(src, b), ACT.Identity, bias=-1.5)
-        tt(blk(dst, b), bank(pb), tmp, ALU.mult, ["pb%d" % pb, tk], [dk], LR)
+    def ntab(src, dst, b, sk, dk, pb, sq, qk):
+        act(LR, sk, qk, sq, blk(src, b), ACT.Square)
+        act(LR, sk, ["pb%d" % pb], bank(pb), blk(src, b), ACT.Identity, bias=-1.5)
+        tt(blk(dst, b), bank(pb), sq, ALU.mult, ["pb%d" % pb] + qk, dk, LR)
 
     for b in range(3):
-        gtab(T.S, T.NG, b, "S%d" % b, "NG%d" % b, b, blk(T.QG, b + 1), "QG%d" % (b + 1))
+        ntab(T.S, T.NG, b, ["S%d" % b], ["NG%d" % b], b, pair(T.SQ, b, 0, LR, 0), un("SQ%d" % b))
+    for p in range(2):
+        snd("G0%d" % p, ["NG0"], 2.0, 10.0)
+    join(["LG00", "LG01"], ["GF00"])
     for b in (1, 2):
-        tmp, tk = (blk(T.QG, 4), "QG4") if b == 1 else (blk(T.M, 3), "M3")
-        act(LR, ["S%d" % b], [tk], tmp, blk(T.S, b), ACT.Square, bias=1.0, scale=-1.0)
-        act(LR, [tk], [tk], tmp, tmp, ACT.Identity, scale=0.5)
-        tt(blk(T.Q, b), bank(b), tmp, ALU.add, ["pb%d" % b, tk], ["Q%d" % b], LR)
-    for b in range(3):
-        gtab(T.SF0, T.GF0, b, "LS0" + "abc"[b], "GF0%d" % b, (3, 4, 7)[b], blk(T.M, b), "M%d" % b)
-    SFK = {0: ["LS0a", "LS0b", "LS0c"], 1: all3("SF1"), 2: all3("SF2")}
-
-    def gather(out, src, n, rd, wr, en=("V", "A")):
-        op(list(en), {"V": tv(n, PAR["g"]), "A": ta(n, PAR["g"])}, rd, wr,
-           lambda q, e: q.tensor_copy(out, src) if e == "V" else q.activation(out, src, ACT.Identity))
+        for (a, n) in HALVES:
+            qk = un("Q%d" % b, a, n)
+            act(n, ["S%d" % b], qk, pair(T.Q, b, a, n, 0), blk(T.S, b, a, n), ACT.Square, bias=1.0, scale=-1.0)
+            act(n, un("SQ%d" % b, a, n), ["pb%d" % b], bank(b, n), pair(T.SQ, b, a, n, 0), ACT.Identity, scale=2.0)
+            tt(pair(T.Q, b, a, n, 1), bank(b, n), pair(T.Q, b, a, n, 0), ALU.add, ["pb%d" % b] + qk, qk, n)
+        join(un("Q%d" % b), ["Q%d" % b])
+    for b in (1, 2):
+        ntab(T.SF0, T.GF0, b, ["SF0%d" % b], ["GF0%d" % b], (7, 3)[b - 1], blk(T.TF, b), ["TF%d" % b])
 
     def spread(tab, key, b, buf, c0, rd):
-        for h in range(2):
-            gather(blk(tab, b, h * LR // 2, LR // 2), T.K[:, 0:V].indirect(buf[:, c0 + 16 * h:c0 + 16 * h + 16]), LR // 2,
-                   KK + rd, ["%s%d%s" % (key, b, "ab"[h])])
+        for h, (a, n) in enumerate(HALVES):
+            gather(blk(tab, b, a, n), by(T.K, buf, c0, a, n), n, KK + rd, ["%s%d%s" % (key, b, "ab"[h])])
 
-    for b in range(3):
-        spread(T.E, "E", b, T.EXW, 32 * b, EXW)
-    dma(["LS0b", "LS0c"], ["SF11", "SF12"], rot(T.SF1, LR, T.SF0, LR, 2 * LR, 1), 5e5)
-    dma(["GF01", "GF02"], ["GF11", "GF12"], rot(T.GF1, LR, T.GF0, LR, 2 * LR, 1), 5e5)
-    dma(["LS0c"], ["SF22"], rot(T.SF2, 2 * LR, T.SF0, 2 * LR, LR, 2), 2.6e5)
-    dma(["GF02"], ["GF22"], rot(T.GF2, 2 * LR, T.GF0, 2 * LR, LR, 2), 2.6e5)
-
-    def wrap(gh, z, pb, n, rd, a=0):
+    def wrap(gh, z, pb, n, rd, start=True):
         def fn(q, e):
             for r in range(16):
-                ins = q.matmul(bank(pb, a, n), T.Z[:, 144 * z + 15 - r:144 * z + 143 - r], gh(r), r == 0, r == 15)
+                ins = q.matmul(bank(pb, n), T.Z[:, 144 * z + 15 - r:144 * z + 143 - r], gh(r), start and r == 0, r == 15)
             return ins
-        op(["P"], {"P": 16 * 64 * PAR["pe"]}, rd + ["Z%d" % z], ["pb%d" % pb], fn, lat=0.1)
+        pe(16 * 64, rd + ["Z%d" % z], pb, fn)
 
-    nlink = [0]
+    EXW = ["EXW0", "EXW32"]
+    for (a, n, pb) in ((0, 32, 6), (32, 64, 5)):
+        wrap(lambda r, a=a, n=n: T.K[:, 16 * a + r:16 * (a + n):16], 0, pb, n, KK)
+        cp(T.EXW[:, a:a + n], bank(pb, n), ["pb%d" % pb], ["EXW%d" % a], n)
+    for b in range(3):
+        spread(T.E, "E", b, T.EXW, 32 * b, ["EXW32" if b else "EXW0"])
+    dma(["SF01", "SF02"], ["SF11", "SF12"], rot(T.SF1, LR, T.SF0, LR, 2 * LR, 1), 5e5)
+    dma(["GF01", "GF02"], ["GF11", "GF12"], rot(T.GF1, LR, T.GF0, LR, 2 * LR, 1), 5e5)
+    dma(["SF02", "GF11"], ["SF22"], rot(T.SF2, 2 * LR, T.SF0, 2 * LR, LR, 2), 2.6e5)
+    dma(["GF02", "GF11"], ["GF22"], rot(T.GF2, 2 * LR, T.GF0, 2 * LR, LR, 2), 2.6e5)
 
-    def offk(o, h, parts_):
-        if o is None:
-            return EXW
-        return ["OFF%d_%d" % (o, hh) for hh in ((0, 1) if parts_ == 1 else (h * 2 // parts_,))]
+    turn = [0, 0]
+
+    def offk(o, a, n):
+        return EXW if o is None else un("OFF%d" % o, a, n)
+
+    def names(flat, c0, fk, outs):
+        for (z, o) in outs:
+            pb = 5 + turn[1] % 2
+            turn[1] += 1
+            wrap(lambda r: flat[:, c0 + r:c0 + LR:16], z, pb, 32, fk)
+            cp(T.OFF[:, 32 * o:32 * o + 32], bank(pb, 32), ["pb%d" % pb], un("OFF%d" % o), 32)
 
     def link(tab, tkeys, buf, c0, o_in, outs):
-        x = nlink[0] % 2
-        nlink[0] += 1
-        for h in range(2):
-            a = x * LR + h * LR // 2
-            gather(T.GH[:, a:a + LR // 2], tab[:, 0:V].indirect(buf[:, c0 + 16 * h:c0 + 16 * h + 16]), LR // 2,
-                   tkeys + offk(o_in, h, 2), ["GH%d_%d" % (x, h)])
-        LH = OPT["LH"]
-        n, w = LR // LH, 32 // LH
-        for h in range(LH):
-            a = x * LR + h * n
-            gk = ["GH%d_%d" % (x, hh) for hh in ((0, 1) if LH == 1 else (h,))]
-            for (z, pb, o) in outs:
-                pb = pb if LH == 1 else 5 + h
-                wrap(lambda r, a=a: T.GH[:, a + r:a + n:16], z, pb, w, gk)
-                cp(T.OFF[:, 32 * o + h * w:32 * o + h * w + w], bank(pb, 0, w), ["pb%d" % pb], offk(o, h, LH), w)
+        x = turn[0] % 2
+        turn[0] += 1
+        for (a, n) in HALVES:
+            gather(blk(T.GH, x, a, n), by(tab, buf, c0, a, n), n, tkeys + offk(o_in, a, n), un("GH%d" % x, a, n))
+        names(T.GH, x * LR, un("GH%d" % x), outs)
 
-    def fetch(tab, tkeys, buf, c0, okeys, j, slot):
-        SPLIT = OPT["SPLIT"] if j > 0 else 2
-        n = LR // SPLIT
-        for h in range(SPLIT):
-            a = j * V + 3 * n * h + slot
-            out = T.D1[:, a:a + 3 * n - 2:3]
-            src = tab[:, 0:V].indirect(buf[:, c0 + h * n // 16:c0 + (h + 1) * n // 16])
-            wr = ["D%d_%d_%d" % (j, slot, hh) for hh in ((0, 1) if SPLIT == 1 else (h * 2 // SPLIT,))]
-            op(["V", "A"], {"V": tv(n, PAR["g"]), "A": ta(n, PAR["g"])}, tkeys + offk(okeys, h, SPLIT), wr,
-               lambda q, e, out=out, src=src: q.tensor_copy(out, src) if e == "V" else q.activation(out, src, ACT.Identity))
+    def fetch(tab, tkeys, buf, c0, o, j, s, pieces):
+        for (a, n) in pieces:
+            gather(slot(T.D1, j, s, a, n), by(tab, buf, c0, a, n), n, tkeys + offk(o, a, n), un("D%d_%d" % (j, s), a, n))
 
-    H = LR // 2
     for t in range(R):
-        SF, GF = T["SF%d" % t], T["GF%d" % t]
-        GFK = all3("GF%d" % t)
-        if t > 0:
-            spread(T.XF, "XF", t - 1, T["LW%d" % t], 0, ["LW%d" % t])
-        tab, tk, z = (T.K, KK, 0) if t == 0 else (T.E, EK, 2)
-        link(tab, tk, T.EXW, 32 * t, None, [(z, 5, 0)])
-        link(tab, tk, T.OFF, 0, 0, [(z, 5, 1)])
-        link(T.E, EK, T.OFF, 32, 1, [(1, 5, 3), (2, 6, 2)])
-        for j in range(3):
-            link(T.XF, XFK, T.OFF, 32 * (3 + j), 3 + j, [(z, 5, 4 + j)])
+        SF, GF, SFK, GFK = T["SF%d" % t], T["GF%d" % t], all3("SF%d" % t), all3("GF%d" % t)
+        St, Qt, u = "S%d" % t, "Q%d" % t, t + 1
         if t == 0:
-            dma(["LX0"], XFK, [(T.XF[4 + y:112:16, :], T.LX[16:128, 96 * y:96 * y + 96]) for y in (0, 1)]
+            names(T.E, 0, ["E0a", "E0b"], [(0, 0)])
+            link(T.E, EK, T.OFF, 0, 0, [(2, 1), (0, 2)])
+            link(T.E, EK, T.OFF, 32, 1, [(1, 3)])
+        else:
+            spread(T.XF, "XF", t - 1, T["LW%d" % t], 0, ["LW%d" % t])
+            link(T.E, EK, T.EXW, 32 * t, None, [(2, 0)])
+            link(T.E, EK, T.OFF, 0, 0, [(2, 1)])
+            link(T.E, EK, T.OFF, 32, 1, [(1, 3), (2, 2)])
+        for j in range(3):
+            link(T.XF, XFK, T.OFF, 32 * (3 + j), 3 + j, [(0 if t == 0 else 2, 4 + j)])
+        if t == 0:
+            dma(["LXh", "LXl"], XFK, [(T.XF[4 + y:112:16, :], T.LX[16:128, 96 * y:96 * y + 96]) for y in (0, 1)]
                 + [(T.XF[116 + y:117 + y, :], T.LX[0:16, 96 * y:96 * y + 96]) for y in (0, 1)], 5e4)
         if t == 1:
             k0, k2 = ["XF0a", "XF0b"], ["XF2a", "XF2b"]
@@ -347,102 +355,85 @@ def build(T):
                 (T.XF[6 + y:112:16, 0:LR], T.XF[20 + y:128:16, 0:LR]), (T.XF[118 + y:119 + y, 0:LR], T.XF[4 + y:5 + y, 0:LR]),
                 (T.XF[4 + y:96:16, 2 * LR:V], T.XF[32 + y:128:16, 2 * LR:V]), (T.XF[100 + y:128:16, 2 * LR:V], T.XF[y:32:16, 2 * LR:V]))], 3e4)
             dma(k0, k0, [(T.XF[4 + y::16, 0:LR], T.XF[6 + y::16, 0:LR]) for y in (0, 1)], 2e4)
-        fetch(GF, GFK, T.OFF, 32 * 6, 6, 0, 0)
-        for j, o in enumerate((5, 4, 3, 2, 1, 0, None)):
-            s, sk, n_, nk = (SF, SFK[t], GF, GFK) if j < 3 else (T.S, all3("S"), T.NG, all3("NG"))
-            buf, c0, ok = (T.OFF, 32 * o, o) if o is not None else (T.EXW, 32 * t, None)
-            fetch(n_, nk, buf, c0, ok, j, 1)
-            fetch(s, sk, buf, c0, ok, j, 2)
-        for j in range(7):
-            for h in range(2):
-                a = 3 * H * h
-                d0, k0 = (T.D0F[:, :], ["D0F0", "D0F1", "D0F2"]) if j == 0 else (T.D0[:, a:a + 3 * H], ["D0c0", "D0c2", "D0s%d" % h])
-                vec(3 * H, 1, k0 + ["D%d_%d_%d" % (j, s, h) for s in range(3)], ["Y%d" % h],
-                    lambda q, e, a=a, d0=d0, j=j: q.tensor_tensor_scan(T.Y[:, a:a + 3 * H], d0, T.D1[:, j * V + a:j * V + a + 3 * H], 0.0, ALU.mult, ALU.add))
-                y = T.Y[:, a + 2:a + 3 * H:3]
-                if j < 6:
-                    b = (j + 1) * V + a
-                    act(H, ["Y%d" % h], ["D0s%d" % h], T.D0[:, a + 1:a + 3 * H - 1:3], y, ACT.Square)
-                    act(H, ["Y%d" % h], ["D%d_0_%d" % (j + 1, h)], T.D1[:, b:b + 3 * H - 2:3], y, ACT.Identity, bias=1.5, scale=-1.0)
+        fetch(GF, GFK, T.OFF, 32 * 6, 6, 0, 0, CHAINS)
+        for j, o in enumerate((4, 3, 2, 1, 0, None), 1):
+            s, sk, g, gk = (SF, SFK, GF, GFK) if j < 3 else (T.S, all3("S"), T.NG, all3("NG"))
+            buf, c0 = (T.OFF, 32 * o) if o is not None else (T.EXW, 32 * t)
+            fetch(g, gk, buf, c0, o, j, 1, WHOLE)
+            fetch(s, sk, buf, c0, o, j, 2, WHOLE if t and o is None else HALVES)
+        act(LR, ["NG%d" % t], un("D7_1"), slot(T.D1, 7, 1, 0, LR), blk(T.NG, t), ACT.Identity)
+        act(LR, [St], un("D7_2"), slot(T.D1, 7, 2, 0, LR), blk(T.S, t), ACT.Identity)
+        for j in range(8):
+            for (a, n) in CHAINS:
+                dk = [un("D%d_%d" % (j, s), a, n) for s in range(3)]
+                yk, y = un("Y", a, n), slot(T.Y, 0, 2, a, n)
+                if j == 0:
+                    d = slot(T.D1, 0, 1, a, n)
+                    tt(d, by(GF, T.OFF, 160, a, n), slot(T.D1, 0, 0, a, n), ALU.subtract, GFK + offk(5, a, n) + dk[0], dk[1], n, FUSED)
+                    tt(y, by(SF, T.OFF, 160, a, n), d, ALU.add, SFK + offk(5, a, n) + dk[1], yk, n, FUSED)
                 else:
-                    act(H, ["Y%d" % h], ["pb%d" % (6 + h)], bank(6 + h, 0, H), y, ACT.Square)
-                    act(H, ["Y%d" % h], ["HL%d" % h], T.HL[:, H * h:H * h + H], y, ACT.Identity, bias=1.5, scale=-1.0)
-        for k in range(5):
-            op(["P"], {"P": LR * PAR["pe"]}, ["WS", "TR"], ["pb%d" % k],
-               lambda q, e, k=k, t=t: q.matmul(bank(k), T.WS[:, 128 * k:128 * k + 128], blk(T.TR, t), True, True), lat=0.1)
-        St = "S%d" % t
-        op([], {}, [], [St], None, kind="j")
-        op([], {}, [], ["Q%d" % t], None, kind="j")
-        for h in range(2):
-            p, pk = bank(6 + h, 0, H), "pb%d" % (6 + h)
-            sl = blk(T.S, t, H * h, H)
-            tt(p, p, T.HL[:, H * h:H * h + H], ALU.mult, [pk, "HL%d" % h], [pk], H)
-            tt(p, p, blk(T.NG, t, H * h, H), ALU.add, [pk, "NG%d" % t], [pk], H)
-            tt(sl, p, sl, ALU.add, [pk, St], [St + "h%d" % h], H)
-        for h in range(2):
-            p, pk = bank(6 + h, 0, H), "pb%d" % (6 + h)
-            sl, sk = blk(T.S, t, H * h, H), St + "h%d" % h
-            sq, vl = T.SQ[:, H * h:H * h + H], T.VL[:, H * h:H * h + H]
-            act(H, [sk], ["VL%d" % h], vl, sl, ACT.Square, bias=1.0, scale=-1.0)
-            act(H, ["VL%d" % h], [pk], p, vl, ACT.Identity, scale=0.5)
-            op(["V", "A"], {"V": tv(H, 2), "A": ta(H)}, [sk], ["SQ%d" % h],
-               lambda q, e, sq=sq, sl=sl: q.tensor_tensor(sq, sl, sl, ALU.mult) if e == "V" else q.activation(sq, sl, ACT.Square))
-            tt(blk(T.Q, t, H * h, H), p, sq, ALU.add, [pk, "SQ%d" % h, "Q%d" % t], ["Q%dh%d" % (t, h)], H)
-        op([], {}, [St + "h0", St + "h1"], [St], None, kind="j")
-        op([], {}, ["Q%dh0" % t, "Q%dh1" % t], ["Q%d" % t], None, kind="j")
+                    scan(T.Y[:, 3 * a:3 * (a + n)], T.D0[:, 3 * a:3 * (a + n)], T.D1[:, j * V + 3 * a:j * V + 3 * (a + n)],
+                         ["D0c0", "D0c2"] + un("D0s", a, n) + dk[0] + dk[1] + dk[2], yk, 3 * n)
+                if j < 7:
+                    act(n, yk, un("D0s", a, n), slot(T.D0, 0, 1, a, n), y, ACT.Square)
+                    act(n, yk, un("D%d_0" % (j + 1), a, n), slot(T.D1, j + 1, 0, a, n), y, ACT.Identity, bias=1.5, scale=-1.0)
+        join([], [St])
+        join([], [Qt])
+        for (a, n) in CHAINS:
+            yk, y, c = un("Y", a, n), slot(T.Y, 0, 2, a, n), 2 * (t * LR + a)
+            act(n, yk + [St], un(St, a, n), blk(T.S, t, a, n), y, ACT.Identity)
+            act(n, yk, un("SQ%d" % t, a, n), pair(T.SQ, t, a, n, 0), y, ACT.Square)
+            act(n, yk, un("VL", a, n), pair(T.SQ, t, a, n, 1), y, ACT.Square, bias=1.0, scale=-1.0)
+            scan(T.Q[:, c:c + 2 * n], T.DQ[:, 0:2 * n], T.SQ[:, c:c + 2 * n], ["DQ", Qt] + un("SQ%d" % t, a, n) + un("VL", a, n), un(Qt, a, n), 2 * n)
+        join(un(St), [St])
+        join(un(Qt), [Qt])
         if t < R - 1:
-            u = t + 1
-            snd("S%d" % u, [St], 6.0)
-            LS, lk = T["LS%d" % u], "LS%d" % u
-            dma([lk], ["SF%d%d" % (u, t)], rot(T["SF%d" % u], t * LR, LS, 0, LR, u), 2.6e5)
-            if t == 0:
-                dma([lk], ["SF20"], rot(T.SF2, 0, LS, 0, LR, 2), 2.6e5)
-        dma([St], [], [(blk(T.ys, t), blk(T.S, t))], 2.6e5)
-        for k in range(5):
-            for (a, n, en) in (((0, H, ["V"]), (H, H, ["A"])) if k == 0 else ((0, LR, ["A"]),)):
-                c = 160 * t + 32 * k + a // 16
-                out, src = blk(T.QG, k, a, n), T.Q[:, 0:V].indirect(T.NBW[:, c:c + n // 16])
-                op(en, {"V": tv(n, PAR["g"]), "A": ta(n, PAR["g"])}, all3("Q") + ["NBW"], ["QG%d" % k if a == 0 else "QG0b"],
-                   lambda q, e, out=out, src=src: q.tensor_copy(out, src) if e == "V" else q.activation(out, src, ACT.Identity))
-        tt(blk(T.M, 0), bank(0), blk(T.QG, 0), ALU.mult, ["pb0", "QG0", "QG0b"], ["M0"], LR)
+            snd("S%d" % u, [St], 3.0, 10.0)
+            dma(["LS%d" % u], ["SF%d%d" % (u, t)], rot(T["SF%d" % u], t * LR, T["LS%d" % u], 0, LR, u), 4e5)
+        dma([St] + (["leftS%d" % u] if t < R - 1 else []), [], [(blk(T.ys, t), blk(T.S, t))], 2.6e5)
+        QK = all3("Q") + ["NBW%d" % t]
+        tt(blk(T.M, 0), by(T.Q, T.NBW, 160 * t, 0, LR), blk(T.W0, t), ALU.mult, QK + ["W0"], ["M0"], LR, FUSED)
         for k in range(1, 5):
-            tt(bank(k), bank(k), blk(T.QG, k), ALU.mult, ["pb%d" % k, "QG%d" % k], ["pb%d" % k], LR)
-            if k < 4:
-                tt(blk(T.M, k), bank(k), blk(T.M, k - 1), ALU.max, ["pb%d" % k, "M%d" % (k - 1)], ["M%d" % k], LR)
-        tt(bank(0), bank(4), blk(T.M, 3), ALU.max, ["pb4", "M3"], ["pb0"], LR)
-        tt(blk(T.AV, 3), blk(T.M, 3), bank(4), ALU.is_ge, ["pb4", "M3"], ["AV3"], LR)
+            w, wk = bank(k - 1), "pb%d" % (k - 1)
+            pe(LR, ["WS", "TR"], k - 1, lambda q, e, w=w, k=k, t=t: q.matmul(w, T.WS[:, 128 * k:128 * k + 128], blk(T.TR, t), True, True))
+            gather(blk(T.QG, k), by(T.Q, T.NBW, 160 * t + 32 * k, 0, LR), LR, QK, ["QG%d" % k])
+            tt(w, w, blk(T.QG, k), ALU.mult, [wk, "QG%d" % k], [wk], LR)
+            tt(blk(T.M, k) if k < 4 else bank(4), w, blk(T.M, k - 1), ALU.max, [wk, "M%d" % (k - 1)], ["M%d" % k if k < 4 else "pb4"], LR)
+        tt(blk(T.AV, 3), blk(T.M, 3), bank(3), ALU.is_ge, ["pb3", "M3"], ["AV3"], LR)
         for k in (2, 0, 1):
-            tt(blk(T.AV, k), blk(T.M, k), bank(0), ALU.is_ge, ["pb0", "M%d" % k], ["AV%d" % k], LR)
-        wrap(lambda r: T.AV[:, 2 * LR + r:4 * LR:16], 3, 6, 64, ["AV2", "AV3"], 0)
-        wrap(lambda r: T.AV[:, r:2 * LR:16], 3, 5, 64, ["AV0", "AV1"], 0)
-        C = T.CODE
-        ck = lambda k: "CODE%d_%d" % (t, k)
-        tt(C[:, t, 64:128], bank(6, 0, 64), C[:, t, 64:128], ALU.add, ["pb6", ck(2), ck(3)], [ck(2), ck(3)], 64)
-        tt(C[:, t, 96:160], C[:, t, 96:160], bank(6, 0, 64), ALU.subtract, ["pb6", ck(3), ck(4)], [ck(3), ck(4)], 64)
-        tt(T.MX[:, 64:96], C[:, t, 96:128], C[:, t, 128:160], ALU.max, [ck(3), ck(4)], ["MX2"], 32)
-        tt(C[:, t, 0:64], bank(5, 0, 64), C[:, t, 0:64], ALU.add, ["pb5", ck(0), ck(1)], [ck(0), ck(1)], 64)
-        tt(C[:, t, 32:96], C[:, t, 32:96], bank(5, 0, 64), ALU.subtract, ["pb5", ck(1), ck(2)], [ck(1), ck(2)], 64)
-        tt(T.MX[:, 32:64], C[:, t, 0:32], T.MX[:, 64:96], ALU.max, [ck(0), "MX2"], ["MX1"], 32)
-        tt(T.MX[:, 0:32], C[:, t, 32:64], C[:, t, 64:96], ALU.max, [ck(1), ck(2)], ["MX0"], 32)
-        tt(T.MI[:, 0:32], T.MX[:, 0:32], T.MX[:, 32:64], ALU.max, ["MX0", "MX1"], ["MI0"], 32)
-        ts(T.MI[:, 32:64], T.MI[:, 0:32], 2047, ALU.bitwise_and, ["MI0"], ["MI1"], 32)
+            tt(blk(T.AV, k), blk(T.M, k), bank(4), ALU.is_ge, ["pb4", "M%d" % k], ["AV%d" % k], LR)
+        for x in (1, 0):
+            pe(64, ["ONE", "CK%d" % x], 5 + x, lambda q, e, x=x: q.matmul(bank(5 + x, 64), T.ONE[0:1, 0:128], T.CK[:, 64 * x:64 * x + 64], True, False))
+            wrap(lambda r, x=x: T.AV[:, 2 * x * LR + r:2 * (x + 1) * LR:16], 3, 5 + x, 64, ["AV%d" % (2 * x), "AV%d" % (2 * x + 1)], False)
+        c = lambda a, b, s=1, t=t: T.CODE[:, 6 * t + a:6 * t + b:s, :]
+        ck = lambda *ks, t=t: ["CODE%d_%d" % (t, k) for k in ks]
+        tt(c(3, 5), bank(6, 64), T.NB[:, t, 64:128], ALU.add, ["pb6", "NB"], ck(3, 4), 64)
+        tt(c(4, 6), c(4, 6), bank(6, 64), ALU.subtract, ["pb6"] + ck(4, 5), ck(4, 5), 64)
+        tt(c(2, 3), c(4, 5), c(5, 6), ALU.max, ck(4, 5), ck(2), 32, 2)
         if t < R - 1:
-            u = t + 1
-            cp(T.XH[:, :], T.MI[:, 32:64], ["MI1"], ["XH"], 32)
-            op(["P"], {"P": 64 * PAR["pe"]}, ["XH", "I2"], ["pb7"],
-               lambda q, e, u=u: q.matmul(bank(7, 0, 32), T.I2[:, 16 * u:16 * u + 128], T.XH[:, :], True, True), lat=0.1)
-            cp(T["RU%d" % u][:, :], bank(7, 0, 32), ["pb7"], ["RU%d" % u], 32)
-            snd("W%d" % u, ["RU%d" % u], 3.5)
+            act(LR, [St], ["pb7"], bank(7), blk(T.S, t), ACT.Identity, bias=-1.5)
+            tt(blk(T.NG, t), bank(7), pair(T.SQ, t, 0, LR, 0), ALU.mult, ["pb7", "AV1"] + un("SQ%d" % t), ["NG%d" % t], LR)
+        tt(c(0, 2), bank(5, 64), T.NB[:, t, 0:64], ALU.add, ["pb5", "NB", "NG%d" % t], ck(0, 1), 64)
+        tt(c(1, 4, 2), c(1, 4, 2), bank(5, 64), ALU.subtract, ["pb5"] + ck(1, 3), ck(1, 3), 64)
+        tt(T.MX[:, :], c(0, 2), c(2, 4), ALU.max, ck(0, 1, 2, 3), ["MX"], 64, 2)
+        tt(T.MI[:, 0:32], T.MX[:, 0:32], T.MX[:, 32:64], ALU.max, ["MX"], ["MI0"], 32, 2)
+        ts(T.MI[:, 32:64], T.MI[:, 0:32], 2047, ALU.bitwise_and, ["MI0"], ["MI1"], 32)
+        cp(T.XO[:, :], T.MI[:, 32:64], ["MI1"], ["XO"], 32)
+        if t < R - 1:
+            pe(256, ["XO", "I2"], 6, lambda q, e, u=u: q.matmul(bank(6, 32), T.I2[:, 16 * u:16 * u + 128], T.XO[:, :], True, True))
+            cp(T["RU%d" % u][:, :], bank(6, 32), ["pb6"], ["RU%d" % u], 32)
+            snd("W%d" % u, ["RU%d" % u], 1.5, 5.5)
             cp(T.NW[:, :], T.MI[:, 32:64], ["MI1"], ["NW"], 32)
             spread(T.E, "E", t, T.NW, 0, ["NW"])
-            act(LR, [St], ["pb2"], bank(2), blk(T.S, t), ACT.Identity, bias=-1.5)
-            tt(blk(T.NG, t), bank(2), T.SQ[:, :], ALU.mult, ["pb2", "SQ0", "SQ1"], ["NG%d" % t], LR)
-            gtab(T["SF%d" % u], T["GF%d" % u], t, "SF%d%d" % (u, t), "GF%d%d" % (u, t), 3, blk(T.M, 0), "M0")
+            ntab(T["LS%d" % u], T.LG, 0, ["LS%d" % u], ["LG"], 0, blk(T.TF, 0), ["TF0"])
+            dma(["LG"], ["GF%d%d" % (u, t)], rot(T["GF%d" % u], t * LR, T.LG, 0, LR, u), 4e5)
             if t == 0:
-                dma(["GF10"], ["GF20"], rot(T.GF2, 0, T.GF1, 0, LR, 1), 2.6e5)
-        cp(T.XO[:, :], T.MI[:, 32:64], ["MI1"], ["XO"], 32)
+                dma(["LG", "GF10"], ["GF20"], rot(T.GF2, 0, T.LG, 0, LR, 2), 2.6e5)
+                dma(["LS1", "GF10"], ["SF20"], rot(T.SF2, 0, T.LS1, 0, LR, 2), 2.6e5)
         vec(32, 1, ["XO"], ["XT%d" % t], lambda q, e, t=t: q.transpose(T.XT[:, 32 * t:32 * t + 32], T.XO[:, :]))
-        dma(["XT%d" % t], [], [(T.yx[q::2, t * LR:t * LR + LR], T.XT[:, 32 * t + 16 * q:32 * t + 16 * q + 16]) for q in (0, 1)], 2e4)
+        for q in (0, 1):
+            dma(["XT%d" % t], [], [(T.yx[q::2, t * LR:t * LR + LR], T.XT[:, 32 * t + 16 * q:32 * t + 16 * q + 16])], 2e4,
+                eng="A" if q and t == R - 1 else "S")
     return ops
 
 
@@ -461,7 +452,7 @@ def edges(ops):
             if k in last:
                 d[last[k]] = True
             for j in readers.get(k, []):
-                d.setdefault(j, False)
+                d[j] = True
         d.pop(i, None)
         deps.append(d)
         for k in o["rd"]:
@@ -472,149 +463,60 @@ def edges(ops):
     return deps
 
 
-def plan(ops, deps):
-    n, SYNC = len(ops), PAR["sy"]
-    rank = [0.0] * n
-    for i in range(n - 1, -1, -1):
-        o = ops[i]
-        rank[i] += (min(o["dur"][e] for e in o["eng"]) if o["eng"] else 0.0) + o["lat"] + 1e-6
-        for j in deps[i]:
-            rank[j] = max(rank[j], rank[i] + SYNC)
-    for i in range(n):
-        if ops[i]["x"] is True:
-            rank[i] = 1e6 - i
-    busy = {e: [] for e in "VAPGS"}
-    start, fin, eng = [0.0] * n, [0.0] * n, [None] * n
-    for i in sorted(range(n), key=lambda i: (-rank[i], i)):
-        o = ops[i]
-        ready = max([fin[j] + SYNC for j in deps[i]] + [0.0])
-        if not o["eng"]:
-            start[i], fin[i] = ready - SYNC, ready - SYNC + o["lat"]
-            continue
-        best = None
-        for e in o["eng"]:
-            s, du = ready, o["dur"][e]
-            for (a, b) in busy[e]:
-                if s + du <= a:
-                    break
-                s = max(s, b)
-            if best is None or s + du < best[0] - 1e-9:
-                best = (s + du, s, e)
-        start[i], eng[i] = best[1], best[2]
-        fin[i] = best[0] + o["lat"]
-        busy[eng[i]].append((best[1], best[0]))
-        busy[eng[i]].sort()
-    return start, fin, eng
-
-
-def place(ops, pre, post, prio, back, pen):
-    n, sy = len(ops), PAR["sy"]
-    busy = {e: [] for e in "VAPGS"}
-    start, fin, eng = [0.0] * n, [0.0] * n, [None] * n
-    left = [len(p) for p in pre]
-    todo = sorted([i for i in range(n) if not left[i]], key=lambda i: -prio[i])
-    while todo:
-        i = todo.pop()
-        o = ops[i]
-        r = 0.0
-        for j in pre[i]:
-            if fin[j] > r:
-                r = fin[j]
-        if not o["eng"]:
-            start[i], fin[i] = r, r + o["lat"]
-        else:
-            r += sy + (o["lat"] if back else 0.0)
-            best = None
-            for e in o["eng"]:
-                s, du, bz = r, o["dur"][e], busy[e]
-                lo, hi = 0, len(bz)
-                while lo < hi:
-                    m = (lo + hi) // 2
-                    if bz[m][1] <= s:
-                        lo = m + 1
-                    else:
-                        hi = m
-                while lo < len(bz) and s + du > bz[lo][0]:
-                    s = bz[lo][1]
-                    lo += 1
-                w = s + du + (pen if e == "V" else 0.0)
-                if best is None or w < best[4] - 1e-9:
-                    best = (s + du, s, e, lo, w)
-            start[i], eng[i] = best[1], best[2]
-            fin[i] = best[0] + (0.0 if back else o["lat"])
-            busy[best[2]].insert(best[3], (best[1], best[0]))
-        new = False
-        for j in post[i]:
-            left[j] -= 1
-            if not left[j]:
-                todo.append(j)
-                new = True
-        if new:
-            todo.sort(key=lambda i: -prio[i])
-    return start, fin, eng, max(fin)
-
-
-def shake(ops, dl, succ, start, rnd):
-    n = len(ops)
-    best = None
-    cur = list(start)
-    for it in range(OPT["PASS"]):
-        for i in range(n):
-            if ops[i]["x"] is True:
-                cur[i] = i - 1e6
-        pen = OPT["PEN"] * rnd(1000) / 1000.0
-        st, fin, eng, end = place(ops, dl, succ, cur, False, pen)
-        if best is None or end < best[3]:
-            best = (st, fin, eng, end)
-        if it % 4 == 3:
-            st, fin = best[0], best[1]
-        amp = OPT["AMP"] * rnd(1000) / 1000.0
-        bs, bf, be, bend = place(ops, succ, dl, [-f + amp * rnd(1000) / 1000.0 for f in fin], True, pen)
-        cur = [-f + amp * rnd(1000) / 1000.0 for f in bf]
-    for it in range(OPT["LNS"]):
-        st, fin, eng, end = best
-        a = rnd(int(end)) - 3.0
-        b = a + 3 + rnd(14)
-        amp, pen = OPT["AMP"] * rnd(1000) / 1000.0, OPT["PEN"] * rnd(1000) / 1000.0
-        loc = [dict(o, eng=o["eng"] if a <= st[i] <= b or eng[i] is None else [eng[i]]) for i, o in enumerate(ops)]
-        nz = lambda i: amp * rnd(1000) / 1000.0 if a <= st[i] <= b else amp / 2
-        if rnd(2):
-            bs, bf, be, bend = place(loc, succ, dl, [-fin[i] + nz(i) for i in range(n)], True, pen)
-            cur = [-bf[i] if a <= st[i] <= b else st[i] + end - bend - end for i in range(n)]
-            cur = [cur[i] if a <= st[i] <= b else st[i] - end for i in range(n)]
-        else:
-            cur = [st[i] + nz(i) for i in range(n)]
-        for i in range(n):
-            if ops[i]["x"] is True:
-                cur[i] = i - 1e6
-        c = place(loc, dl, succ, cur, False, pen)
-        if c[3] <= end + 1e-9:
-            best = c
-    return best
-
-
-def replay(seq, eng, dl, dur, lat, sy):
-    fin = [0.0] * len(dl)
-    start = [0.0] * len(dl)
-    free = {"V": 0.0, "A": 0.0, "P": 0.0, "G": 0.0, "S": 0.0}
-    for i in seq:
+def run(seq, a, eng, dl, dur, lat, sy, fin, end):
+    free = {"V": 0.0, "A": 0.0, "P": 0.0, "G": 0.0, "S": 0.0, None: 0.0}
+    for i in seq[:a]:
+        free[eng[i]] = end[i]
+    for i in seq[a:]:
         r = 0.0
         for j in dl[i]:
             if fin[j] > r:
                 r = fin[j]
         e = eng[i]
-        if e is None:
-            start[i] = r
-            fin[i] = r + lat[i]
-        else:
+        if e is not None:
             r += sy
             if free[e] > r:
                 r = free[e]
-            start[i] = r
             r += dur[i][e]
             free[e] = r
-            fin[i] = r + lat[i]
-    return max(fin), start
+        end[i] = r
+        fin[i] = r + lat[i]
+    return max(fin) + OPT["PULL"] * sum(fin) / len(fin)
+
+
+def pack(win, ops, dl, succ, prio, pen, free, fin, eng, back=False):
+    sy, inw = PAR["sy"], set(win)
+    busy = {e: [(0.0, free[e])] for e in "VAPGS"}
+    left = {i: sum(j in inw for j in dl[i]) for i in win}
+    todo = [i for i in win if not left[i]]
+    start = {}
+    while todo:
+        i = min(todo, key=prio.get)
+        todo.remove(i)
+        o = ops[i]
+        r = max([fin[j] for j in dl[i]] + [0.0])
+        if not o["eng"]:
+            start[i], fin[i] = r, r + o["lat"]
+        else:
+            best = None
+            for e in o["eng"]:
+                s, du, k = r + sy + (o["lat"] if back else 0.0), o["dur"][e], 0
+                for k, (x, y) in enumerate(busy[e] + [(1e9, 1e9)]):
+                    if s + du <= x:
+                        break
+                    s = max(s, y)
+                w = s + du + (pen if e == "V" else 0.0)
+                if best is None or w < best[0]:
+                    best = (w, s, e, k)
+            w, s, e, k = best
+            start[i], eng[i], fin[i] = s, e, s + o["dur"][e] + (0.0 if back else o["lat"])
+            busy[e].insert(k, (s, s + o["dur"][e]))
+        for j in succ[i]:
+            if j in inw:
+                left[j] -= 1
+                if not left[j]:
+                    todo.append(j)
+    return sorted(win, key=lambda i: (start[i], i))
 
 
 def arrange(T):
@@ -626,59 +528,66 @@ def arrange(T):
     PAR.update(PARS[0])
     ops = build(T)
     deps = edges(ops)
-    start, fin, eng = plan(ops, deps)
     n = len(ops)
     dl = [list(d) for d in deps]
     succ = [[] for o in ops]
-    for i in range(n):
+    rank = [0.0] * n
+    for i in range(n - 1, -1, -1):
+        o = ops[i]
+        rank[i] += min([o["dur"][e] for e in o["eng"]] or [0.0]) + o["lat"]
         for j in dl[i]:
             succ[j].append(i)
+            rank[j] = max(rank[j], rank[i] + PAR["sy"])
     x = [OPT["SEED"]]
 
-    def rnd(m):
+    def rnd():
         x[0] = (x[0] * 6364136223846793005 + 1442695040888963407) % (1 << 64)
-        return (x[0] >> 33) % m
+        return (x[0] >> 33) / float(1 << 31)
 
-    start, fin, eng, end = shake(ops, dl, succ, start, rnd)
-    seq = sorted(range(n), key=lambda i: (start[i], i))
-    base = [replay(seq, eng, dl, *s)[0] for s in sets]
-
-    def score(sq, en):
-        return sum(replay(sq, en, dl, *s)[0] / b for s, b in zip(sets, base))
-
-    best = score(seq, eng)
     first = [i for i in range(n) if ops[i]["x"] is True]
-    mov = [i for i in range(n) if eng[i] is not None and i not in first]
-    for step in range(OPT["STEPS"]):
-        i = mov[rnd(len(mov))]
-        en = eng
-        if len(ops[i]["eng"]) > 1 and rnd(2) == 0:
-            en = list(eng)
-            en[i] = [e for e in ops[i]["eng"] if e != eng[i]][0]
-        p = seq.index(i)
-        sq = seq[:p] + seq[p + 1:]
-        k = rnd(3) + (0 if en is not eng else 1)
-        if rnd(2):
-            q, stop = p, set(dl[i] + first)
-            while q > 0 and k > 0 and sq[q - 1] not in stop:
-                q -= 1
-                k -= en[sq[q]] == en[i]
-        else:
-            q, stop = p, set(succ[i])
-            while q < n - 1 and k > 0 and sq[q] not in stop:
-                k -= en[sq[q]] == en[i]
-                q += 1
-        if q == p and en is eng:
-            continue
-        sq.insert(q, i)
-        s = score(sq, en)
-        if s <= best:
-            best, seq, eng = s, sq, en
-            if step % 8 == 0:
-                st = replay(seq, eng, dl, *sets[0])[1]
-                pos = {j: a for a, j in enumerate(seq)}
-                seq = sorted(seq, key=lambda j: (st[j], pos[j]))
-    return deps, seq, eng, [replay(seq, eng, dl, *s)[0] for s in sets], base
+    eng = [None] * n
+    seq = pack(list(range(n)), ops, dl, succ, {i: i - 1e6 if i in first else -rank[i] for i in range(n)}, 0.0,
+               dict.fromkeys("VAPGS", 0.0), [0.0] * n, eng)
+    seq = first + [i for i in seq if i not in first]
+    times = [([0.0] * n, [0.0] * n) for s in sets]
+    base = [run(seq, 0, eng, dl, *s, *t) for s, t in zip(sets, times)]
+    weight = [w / b for w, b in zip(OPT["WEIGHT"], base)]
+    best, now = sum(OPT["WEIGHT"]), base[0]
+    keep = (best, seq, eng)
+    for it in range(OPT["TRIES"]):
+        a = len(first) + int(rnd() * (n - len(first) - 10))
+        win = seq[a:a + 10 + int(rnd() * OPT["WIN"])]
+        fin, end = times[0]
+        free = dict.fromkeys("VAPGS", 0.0)
+        for i in seq[:a]:
+            free[eng[i]] = end[i]
+        amp, mix = OPT["AMP"] * rnd(), rnd() < 0.3
+        prio = {i: (-rank[i] if mix else end[i]) + amp * rnd() for i in win}
+        en = list(eng)
+        if rnd() < OPT["BACK"]:
+            top = max(fin)
+            rev = [top - end[i] + (ops[i]["dur"][eng[i]] if eng[i] else 0.0) for i in range(n)]
+            after = dict.fromkeys("VAPGS", 0.0)
+            for i in reversed(seq[a + len(win):]):
+                after[eng[i]] = rev[i]
+            pack(win, ops, succ, dl, {i: amp * rnd() - fin[i] for i in win}, OPT["PEN"] * rnd() * rnd(), after, rev, list(eng), True)
+            prio = {i: amp * rnd() * 0.5 - rev[i] for i in win}
+        sq = seq[:a] + pack(win, ops, dl, succ, prio, OPT["PEN"] * rnd() * rnd(), free, list(fin), en) + seq[a + len(win):]
+        limit = best + OPT["HEAT"] * (1.0 - it / OPT["TRIES"]) * rnd() * rnd()
+        tm, vs = [], []
+        for st, t in zip(sets, times):
+            tm.append((list(t[0]), list(t[1])))
+            vs.append(run(sq, a, en, dl, *st, *tm[-1]))
+            if vs[0] > now + 0.5:
+                break
+        s = sum(w * v for w, v in zip(weight, vs))
+        if len(vs) == len(sets) and s <= limit:
+            best, now, eng, times = s, vs[0], en, tm
+            pos = {j: k for k, j in enumerate(sq)}
+            seq = first + sorted(sq[len(first):], key=lambda j: (tm[0][1][j] - (ops[j]["dur"][en[j]] if en[j] else 0.0), pos[j]))
+            if s < keep[0]:
+                keep = (s, seq, eng)
+    return deps, keep[1], keep[2]
 
 
 PLAN = {}
@@ -687,14 +596,14 @@ PLAN = {}
 def rank_program(g, core, T, topo):
     rank = T.rank_of(core)
     if rank is None:
-        helper_program(g, core, T, topo)
+        relay_program(g, core, T, topo)
         return
     n = len(T.cores)
     dst, src = T.cores[(rank - 1) % n], T.cores[(rank + 1) % n]
     if not PLAN:
         PLAN["plan"] = arrange(T)
     ops = build(T)
-    deps, seq, eng = PLAN["plan"][:3]
+    deps, seq, eng = PLAN["plan"]
     Qs = {"V": g.vector, "A": g.scalar, "P": g.tensor, "G": g, "S": g.sync}
     clock = {e: {} for e in Qs}
     count = {}
@@ -704,7 +613,7 @@ def rank_program(g, core, T, topo):
         o, e = ops[i], eng[i]
         if o["kind"] == "a":
             m = o["x"]
-            c = arrivals(T, topo, src, core, message(T, m)[5])
+            c = arrivals(T, topo, src, core, m)
             count["a" + m] = c
             tok[i] = [("a" + m, c, {}, None)]
             continue

from concourse.bass import DstId, RemoteDMATransfer
from concourse.mybir import AluOpType as ALU, ActivationFunctionType as ACT

V, LR, R = 1536, 512, 3
H = LR // 2
F32, I32, U16, BF = "float32", "int32", "uint16", "bfloat16"
SCRATCH = {
    "S": ("sbuf", [128, V], F32), "NG": ("sbuf", [128, V], F32), "Q": ("sbuf", [128, 2 * V], F32), "SQ": ("sbuf", [128, 2 * V], F32),
    "SF0": ("sbuf", [128, V], F32), "SF1": ("sbuf", [128, V], F32), "SF2": ("sbuf", [128, V], F32),
    "GF0": ("sbuf", [128, V], F32), "GF1": ("sbuf", [128, V], F32), "GF2": ("sbuf", [128, V], F32),
    "K": ("sbuf", [128, V], BF), "E": ("sbuf", [128, V], BF), "XF": ("sbuf", [128, V], BF),
    "CM": ("sbuf", [128, 96], I32), "CW": ("sbuf", [128, 384], I32), "HB": ("sbuf", [128, 768], BF),
    "D1": ("sbuf", [128, 8 * V], F32), "D0": ("sbuf", [128, V], F32), "Y": ("sbuf", [128, V], F32), "DQ": ("sbuf", [128, LR], F32),
    "LS1": ("sbuf", [128, LR], F32), "LS2": ("sbuf", [128, LR], F32), "LG": ("sbuf", [128, LR], F32), "TF": ("sbuf", [128, V], F32),
    "LW1": ("sbuf", [128, 32], U16), "LW2": ("sbuf", [128, 32], U16), "LX": ("sbuf", [128, 192], BF), "LI": ("sbuf", [128, 96], I32),
    "QG": ("sbuf", [128, 5 * LR], F32), "M": ("sbuf", [128, 4 * LR], F32), "AV": ("sbuf", [128, 4 * LR], BF),
    "GH": ("sbuf", [128, 2 * LR], BF), "OFF": ("sbuf", [128, 7 * 32], U16), "EXW": ("sbuf", [128, 96], U16),
    "NIL": ("sbuf", [128, LR], BF), "CK": ("sbuf", [1, 128], BF), "W0": ("sbuf", [128, V], BF),
    "NB": ("sbuf", [128, 3, 160], I32), "NBW": ("sbuf", [128, 480], U16), "CODE": ("sbuf", [128, 18, 32], F32),
    "TR": ("sbuf", [40, V], BF), "ONE": ("sbuf", [40, 640], BF), "WS": ("sbuf", [40, 640], BF),
    "DZ": ("sbuf", [128, 144], F32), "PC": ("sbuf", [128, 4], I32), "PF": ("sbuf", [128, 12], F32),
    "ZB": ("sbuf", [128, 144], BF), "Z": ("sbuf", [128, 4 * 144], BF),
    "D2": ("sbuf", [128, 160], I32), "I2": ("sbuf", [128, 160], F32),
    "MX": ("sbuf", [128, 64], F32), "MI": ("sbuf", [128, 64], I32), "NW": ("sbuf", [128, 32], U16),
    "RU1": ("sbuf", [128, 32], U16), "RU2": ("sbuf", [128, 32], U16),
    "XO": ("sbuf", [128, 32], F32), "XT": ("sbuf", [128, 96], F32),
    "PS": ("psum", [128, 8 * LR], F32),
}
MSGS = ["X0"] + ["S0%d" % p for p in range(6)] + ["G00", "G01", "S1", "W1", "S2", "W2"]
NDMA = 40
SEMAPHORES = ["cV", "cA", "cP", "cG"] + ["a" + m for m in MSGS] + ["l" + m for m in MSGS] + ["d%d" % i for i in range(NDMA)]
CHAINS = [(0, 192), (192, 160), (352, 160)]

CYC = 0.83e-3
PARS = [
    {"f": 1.05, "g": 1.56, "pe": 0.5e-3, "sy": 0.11, "dl": 1.6, "bw": 4e5, "rl": 0.65},
    {"f": 1.35, "g": 1.95, "pe": 0.57e-3, "sy": 0.08, "dl": 1.7, "bw": 3e5, "rl": 0.75},
    {"f": 1.0, "g": 1.2, "pe": 0.5e-3, "sy": 0.15, "dl": 1.8, "bw": 3e5, "rl": 0.75},
]
PAR = dict(PARS[0])
OPT = {"TRIES": 24000, "SEED": 5, "WIN": 110, "HEAT": 0.008, "BACK": 0.8, "AMP": 1.2, "PEN": 1.5, "PULL": 0.01, "WEIGHT": [2, 1, 1]}


def tv(n, c=1.0, f0=0.055):
    return PAR["f"] * (f0 + n * c * CYC)


def ta(n, c=1.0):
    return tv(n, c, 0.065)


def message(T, m):
    if m == "X0":
        return T.CM, 0, T.LI, 0, 96
    if m[0] == "W":
        return T["RU" + m[1]], 0, T["LW" + m[1]], 0, 32
    if m[1] == "0":
        c = int(m[2]) * H
        return (T.S, c, T.SF0, c, H) if m[0] == "S" else (T.NG, c, T.GF0, c, H)
    return T.S, (int(m[1]) - 1) * LR, T["LS" + m[1]], 0, LR


def bits(mask):
    return bin(mask).count("1")


def legs(T, topo, src, dst, m):
    if topo.may_write(src, dst):
        return [(dst, topo.mask(src, dst))]
    near = [c for c in topo.cores_of(src) if T.rank_of(c) is None and topo.may_write(c, dst)]
    near = [c for c in near if all(topo.die(x) != topo.die(c) for x in near if x < c)]
    near.sort(key=lambda c: topo.die(c) != topo.die(src))
    if m[0] == "W" or len(m) == 3:
        c = near[int(m[2]) % len(near) if len(m) == 3 else 0]
        return [(c, topo.mask(src, c))]
    es = topo.engines(src, near[0])
    k = len(es) // len(near)
    return [(c, sum(1 << e for e in es[i * k:(i + 1) * k])) for i, c in enumerate(near)]


def arrivals(T, topo, src, dst, m):
    return sum(bits(mask if c == dst else topo.mask(c, dst)) for c, mask in legs(T, topo, src, dst, m))


def send(g, T, topo, src, dst, m):
    sb, so, lb, lo, n = message(T, m)
    ls = legs(T, topo, src, dst, m)
    w = n // len(ls)
    sides = [(lb[:, lo + i * w:lo + (i + 1) * w], sb[:, so + i * w:so + (i + 1) * w]) for i in range(len(ls))]
    if len(ls) == 1:
        rid, pid = topo.addr(ls[0][0], src)
        g.remote_dma(sides[0][0], sides[0][1], T.sem["a" + m], T.sem["l" + m], pid, rid, ls[0][1])
    else:
        g.remote_dma_fused([RemoteDMATransfer(dst_ids=[DstId(rid=topo.addr(c, src)[0], pnc=topo.addr(c, src)[1])], dma_engine_mask=mask,
                                              remote_sem=T.sem["a" + m], src=s, dst=o) for (c, mask), (o, s) in zip(ls, sides)],
                           local_sem=T.sem["l" + m])
    return sum(bits(mask) for c, mask in ls)


def relay_program(g, core, T, topo):
    n = len(T.cores)
    sent = []
    for m in MSGS:
        for r in range(n):
            src, dst = T.cores[r], T.cores[(r - 1) % n]
            ls = legs(T, topo, src, dst, m)
            for i, (c, got) in enumerate(ls):
                if c == core:
                    sb, so, lb, lo, w = message(T, m)
                    w //= len(ls)
                    piece = lb[:, lo + i * w:lo + (i + 1) * w]
                    rid, pid = topo.addr(dst, core)
                    g.wait_ge(T.sem["a" + m], bits(got))
                    g.remote_dma(piece, piece, T.sem["a" + m], T.sem["l" + m], pid, rid, topo.mask(core, dst))
                    sent.append((m, bits(topo.mask(core, dst))))
    for m, c in sent:
        g.wait_ge(T.sem["l" + m], c)


def build(T):
    ops = []

    def op(eng, dur, rd, wr, fn, lat=0.0, kind="c", extra=None):
        ops.append({"eng": eng, "dur": dur, "rd": rd, "wr": wr, "fn": fn, "lat": lat, "kind": kind, "x": extra})

    def join(rd, wr, lat=0.0):
        op([], {}, rd, wr, None, lat=lat, kind="j")

    def vec(n, c, rd, wr, fn):
        op(["V"], {"V": tv(n, c)}, rd, wr, fn)

    def act(n, rd, wr, out, in_, func, bias=0.0, scale=1.0):
        def fn(q, e):
            if e == "A":
                return q.activation(out, in_, func, bias=bias, scale=scale)
            if func == ACT.Square:
                return q.tensor_tensor(out, in_, in_, ALU.mult)
            return q.tensor_scalar(out, in_, scale, bias, ALU.mult, ALU.add)
        both = func == ACT.Identity or bias == 0.0
        op(["A", "V"] if both else ["A"], {"A": ta(n), "V": tv(n, 2 if func == ACT.Square else 1)}, rd, wr, fn)

    def dma(rd, wr, pairs, nbytes, eng="S", first=False):
        op([eng], {eng: 0.1 * len(pairs)}, rd, wr, pairs, lat=PAR["dl"] + nbytes / PAR["bw"], kind="d", extra=first)

    def pool(dur, rd, wr, fn):
        op(["G"], {"G": dur * PAR["f"]}, rd, wr, fn)

    def fill(ap, pattern, base, n, wr):
        pool(0.13 + 2 * n * CYC, ["sentS05"], wr, lambda q, e: q.iota(ap, pattern, base, 0, allow_small_or_imprecise_dtypes=True))

    def clear(ap, wr):
        op(["A"], {"A": ta(LR)}, ["NIL"], wr, lambda q, e: q.activation(ap, T.NIL[:, :], ACT.Identity))

    def pe(cycles, rd, pb, fn):
        op(["P"], {"P": cycles * PAR["pe"]}, rd, ["pb%d" % pb], fn, lat=0.1)

    def snd(m, rd, left, landed):
        op(["G"], {"G": 2.3 if m == "X0" else 0.3}, rd, ["sent" + m, "order"], None, kind="s", extra=m)
        op([], {}, ["sent" + m], ["L" + m], None, lat=landed * PAR["rl"], kind="a", extra=m)
        join(["sent" + m], ["left" + m], left * PAR["rl"])

    def bank(b, n=LR):
        return T.PS[:, b * LR:b * LR + n]

    def blk(t, b, a=0, n=LR):
        return t[:, b * LR + a:b * LR + a + n]

    def pair(buf, b, a, n, s):
        return buf[:, 2 * (b * LR + a) + s:2 * (b * LR + a + n) - 1 + s:2]

    def slot(buf, j, s, a, n):
        return buf[:, j * V + 3 * a + s:j * V + 3 * (a + n) - 2 + s:3]

    def tt(out, a, b, o, rd, wr, n, c=1.0):
        vec(n, c, rd, wr, lambda q, e: q.tensor_tensor(out, a, b, o))

    def ts(out, a, s, o, rd, wr, n, c=1.0):
        vec(n, c, rd, wr, lambda q, e: q.tensor_scalar(out, a, s, None, o))

    def cp(out, a, rd, wr, n):
        vec(n, 1, rd, wr, lambda q, e: q.tensor_copy(out, a))

    def scan(out, d0, d1, rd, wr, n):
        vec(n, 1, rd, wr, lambda q, e: q.tensor_tensor_scan(out, d0, d1, 0.0, ALU.mult, ALU.add))

    def gather(out, src, n, rd, wr):
        op(["V", "A"], {"V": tv(n, PAR["g"]), "A": ta(n, PAR["g"])}, rd, wr,
           lambda q, e: q.tensor_copy(out, src) if e == "V" else q.activation(out, src, ACT.Identity))

    def by(tab, buf, c0, a, n):
        return tab[:, :].indirect(buf[:, c0 + a // 16:c0 + (a + n) // 16])

    def rot(dst, dc, src, sc, n, t):
        s = 16 * t
        return [(dst[0:128 - s, dc:dc + n], src[s:128, sc:sc + n]), (dst[128 - s:128, dc:dc + n], src[0:s, sc:sc + n])]

    def all3(k):
        return [k + "0", k + "1", k + "2"]

    def un(name, a=0, n=LR):
        return ["%s.%d" % (name, u) for u in range(a // 32, (a + n) // 32)]

    def split(a, hi, lo, n, keys, out):
        cp(hi, a, keys, [out + "h"], n)
        tt(lo, a, hi, ALU.subtract, keys + [out + "h"], [out + "l"], n, 2)

    WHOLE, HALVES = [(0, LR)], [(0, H), (H, H)]
    FUSED = max(2, PAR["g"])
    dma([], ["CM0"], [(T.CM[:, :], T.ex[:, :])], 5e4, eng="A", first=True)
    dma([], ["CW0"], [(T.CW[0:64, 0:192], T.ex[:, :])], 1e5, first=True)
    dma([], ["CW1"], [(T.CW[64:128, 0:192], T.pt[:, :])], 1e5, eng="A", first=True)
    for b in range(2):
        dma([], ["S%d" % b], [(blk(T.S, b), blk(T.sat, b))], 2.6e5 * (b + 1.5), first=True)
    pool(0.13 + 384 * CYC, [], ["CW2"], lambda q, e: q.iota(T.CW[0:64, 192:384], [[1, 192]], 0, 0))
    pool(0.14, [], ["PC0"], lambda q, e: q.iota(T.PC[:, 0:1], [[1, 1]], 0, 1))
    ts(T.PC[:, 1:2], T.PC[:, 0:1], 15, ALU.bitwise_and, ["PC0"], ["PC1"], 1)
    cp(T.PF[:, 0:1], T.PC[:, 1:2], ["PC1"], ["PF0"], 1)
    ts(T.PC[:, 3:4], T.PC[:, 0:1], 7, ALU.bitwise_and, ["PC0"], ["PC3"], 1)
    ts(T.PF[:, 8:9], T.PC[:, 3:4], 192.0, ALU.mult, ["PC3"], ["PF8"], 1)
    ts(T.CW[0:64, 192:384], T.CW[0:64, 192:384], T.PF[0:64, 8:9], ALU.add, ["CW2", "PF8"], ["CW2"], 192)
    op(["V"], {"V": tv(LR, 0.5)}, [], ["NIL"], lambda q, e: q.memset(T.NIL[:, :], 0.0), extra=True)
    for b in range(3):
        clear(blk(T.K, b), ["Kz%d" % b])
    join(all3("Kz"), ["K"])
    split(T.CW[0:64, 192:384], T.HB[0:64, 384:576], T.HB[0:64, 576:768], 192, ["CW2"], "HI")
    dma(["K", "HIh", "HIl"], ["K2"], [(T.K[4 + y::16, :], T.HB[0:64, 384 + 192 * y:576 + 192 * y]) for y in (0, 1)], 1e5)
    split(T.CW[:, 0:192], T.HB[:, 0:192], T.HB[:, 192:384], 192, ["CW0", "CW1", "HIl"], "HB")
    for x in range(2):
        dma(["K", "HBh", "HBl"], ["K%d" % x],
            [(T.K[2 * x + y::16, :], T.HB[64 * x:64 * x + 64, 192 * y:192 * y + 192]) for y in (0, 1)], 3e5)
    KK = all3("K")
    snd("X0", ["CM0"], 1.2, 6.0)
    join(["HBl"], ["late"], 0.6)
    dma(["late"], ["S2"], [(blk(T.S, 2), blk(T.sat, 2))], 5.2e5)
    for p, landed in enumerate((8, 8.5, 9, 9.5, 8.5, 9)):
        snd("S0%d" % p, ["S%d" % (p // 2)], 2.0, landed)
    for b in range(3):
        join(["LS0%d" % (2 * b), "LS0%d" % (2 * b + 1)], ["SF0%d" % b])
        clear(blk(T.XF, b), ["XF%da" % b, "XF%db" % b])
    XFK = [k + s for k in all3("XF") for s in "ab"]
    EK = [k + s for k in all3("E") for s in "ab"]
    split(T.LI[:, :], T.LX[:, 0:96], T.LX[:, 96:192], 96, ["LX0"], "LX")
    dma(["LXh", "LXl"], XFK, [(T.XF[y::16, :], T.LX[:, 96 * y:96 * y + 96]) for y in (0, 1)], 3e5)
    dma(XFK, ["NB"], [(T.NB[:], T.nb[:, :])], 8e5)
    dma(XFK, ["TR"], [(T.TR[:, :], T.tr[:, :])], 8e5)
    dma(["TR"], ["W0"], [(T.W0[p::16, :], T.tr[0::5, :]) for p in range(16)], 8e5)
    pool(0.37, [], ["DZ"], lambda q, e: q.iota(T.DZ[:, :], [[1, 144]], 0, -1, allow_small_or_imprecise_dtypes=True))
    pool(0.14, [], ["PF1"], lambda q, e: q.iota(T.PF[:, 1:4], [[1, 3]], 0, 0, allow_small_or_imprecise_dtypes=True))
    ts(T.PC[:, 2:3], T.PC[:, 1:2], 1, ALU.arith_shift_right, ["PC1"], ["PC2"], 1)
    cp(T.PF[:, 7:8], T.PC[:, 2:3], ["PC2"], ["PF7"], 1)
    ts(T.PF[:, 4:7], T.PF[:, 1:4], T.PF[:, 7:8], ALU.is_equal, ["PF7", "PF1"], ["PF4"], 3)
    vec(144, 1, ["DZ", "PF0"], ["ZB"], lambda q, e: q.tensor_scalar(T.ZB[:, :], T.DZ[:, :], T.PF[:, 0:1], 15.0, ALU.add, ALU.is_equal))
    for z in range(3):
        ts(T.Z[:, 144 * z:144 * z + 144], T.ZB[:, :], T.PF[:, 4 + z:5 + z], ALU.mult, ["ZB", "PF4"], ["Z%d" % z], 144, 0.5)
    ts(T.Z[:, 432:576], T.ZB[:, :], 16384.0, ALU.mult, ["ZB"], ["Z3"], 144, 0.5)
    pool(0.4, [], ["D2"], lambda q, e: q.iota(T.D2[:, :], [[1, 160]], 128, -1))
    ts(T.D2[:, :], T.D2[:, :], 127, ALU.bitwise_and, ["D2"], ["D2"], 160)
    ts(T.I2[:, :], T.D2[:, :], 0.0, ALU.is_equal, ["D2"], ["I2"], 160)
    fill(T.ONE[:, :], [[0, 640]], 1, 640, ["ONE"])
    pool(0.17 + 1280 * CYC, ["ONE"], ["WS"], lambda q, e: q.affine_select(T.WS[:, :], T.ONE[:, :], [[-1, 5], [-5, 8], [0, 16]], ALU.is_equal, 0.0, 0, 1))
    fill(T.D0[:, 0::3], [[0, LR]], 0, LR, ["D0c0"])
    fill(T.D0[:, 2::3], [[0, LR]], 1, LR, ["D0c2"])
    fill(T.DQ[:, :], [[0, H], [2, 2]], 0, LR, ["DQ"])
    for t in range(R):
        vec(160, 1, ["NB"], ["NBW%d" % t], lambda q, e, t=t: q.tensor_scalar(T.NBW[:, 160 * t:160 * t + 160], T.NB[:, t, :], 2.0, 1.0, ALU.mult, ALU.add))
    for c, (base, step) in enumerate(((7, 6), (18, 4))):
        fill(T.CK[:, 64 * c:64 * c + 64], [[step * 2048, 2], [0, 32]], base * 2048, 64, ["CK%d" % c])
    ts(T.CODE[:, 5::6, :], T.NB[:, :, 128:160], float(25 * 2048 + 16 * 16384), ALU.add, ["NB"], ["CODE%d_5" % t for t in range(R)], 96)

    def ntab(src, dst, b, sk, dk, pb, sq, qk):
        act(LR, sk, qk, sq, blk(src, b), ACT.Square)
        act(LR, sk, ["pb%d" % pb], bank(pb), blk(src, b), ACT.Identity, bias=-1.5)
        tt(blk(dst, b), bank(pb), sq, ALU.mult, ["pb%d" % pb] + qk, dk, LR)

    for b in range(3):
        ntab(T.S, T.NG, b, ["S%d" % b], ["NG%d" % b], b, pair(T.SQ, b, 0, LR, 0), un("SQ%d" % b))
    for p in range(2):
        snd("G0%d" % p, ["NG0"], 2.0, 10.0)
    join(["LG00", "LG01"], ["GF00"])
    for b in (1, 2):
        for (a, n) in HALVES:
            qk = un("Q%d" % b, a, n)
            act(n, ["S%d" % b], qk, pair(T.Q, b, a, n, 0), blk(T.S, b, a, n), ACT.Square, bias=1.0, scale=-1.0)
            act(n, un("SQ%d" % b, a, n), ["pb%d" % b], bank(b, n), pair(T.SQ, b, a, n, 0), ACT.Identity, scale=2.0)
            tt(pair(T.Q, b, a, n, 1), bank(b, n), pair(T.Q, b, a, n, 0), ALU.add, ["pb%d" % b] + qk, qk, n)
        join(un("Q%d" % b), ["Q%d" % b])
    for b in (1, 2):
        ntab(T.SF0, T.GF0, b, ["SF0%d" % b], ["GF0%d" % b], (7, 3)[b - 1], blk(T.TF, b), ["TF%d" % b])

    def spread(tab, key, b, buf, c0, rd):
        for h, (a, n) in enumerate(HALVES):
            gather(blk(tab, b, a, n), by(T.K, buf, c0, a, n), n, KK + rd, ["%s%d%s" % (key, b, "ab"[h])])

    def wrap(gh, z, pb, n, rd, start=True):
        def fn(q, e):
            for r in range(16):
                ins = q.matmul(bank(pb, n), T.Z[:, 144 * z + 15 - r:144 * z + 143 - r], gh(r), start and r == 0, r == 15)
            return ins
        pe(16 * 64, rd + ["Z%d" % z], pb, fn)

    EXW = ["EXW0", "EXW32"]
    for (a, n, pb) in ((0, 32, 6), (32, 64, 5)):
        wrap(lambda r, a=a, n=n: T.K[:, 16 * a + r:16 * (a + n):16], 0, pb, n, KK)
        cp(T.EXW[:, a:a + n], bank(pb, n), ["pb%d" % pb], ["EXW%d" % a], n)
    for b in range(3):
        spread(T.E, "E", b, T.EXW, 32 * b, ["EXW32" if b else "EXW0"])
    dma(["SF01", "SF02"], ["SF11", "SF12"], rot(T.SF1, LR, T.SF0, LR, 2 * LR, 1), 5e5)
    dma(["GF01", "GF02"], ["GF11", "GF12"], rot(T.GF1, LR, T.GF0, LR, 2 * LR, 1), 5e5)
    dma(["SF02", "GF11"], ["SF22"], rot(T.SF2, 2 * LR, T.SF0, 2 * LR, LR, 2), 2.6e5)
    dma(["GF02", "GF11"], ["GF22"], rot(T.GF2, 2 * LR, T.GF0, 2 * LR, LR, 2), 2.6e5)

    turn = [0, 0]

    def offk(o, a, n):
        return EXW if o is None else un("OFF%d" % o, a, n)

    def names(flat, c0, fk, outs):
        for (z, o) in outs:
            pb = 5 + turn[1] % 2
            turn[1] += 1
            wrap(lambda r: flat[:, c0 + r:c0 + LR:16], z, pb, 32, fk)
            cp(T.OFF[:, 32 * o:32 * o + 32], bank(pb, 32), ["pb%d" % pb], un("OFF%d" % o), 32)

    def link(tab, tkeys, buf, c0, o_in, outs):
        x = turn[0] % 2
        turn[0] += 1
        for (a, n) in HALVES:
            gather(blk(T.GH, x, a, n), by(tab, buf, c0, a, n), n, tkeys + offk(o_in, a, n), un("GH%d" % x, a, n))
        names(T.GH, x * LR, un("GH%d" % x), outs)

    def fetch(tab, tkeys, buf, c0, o, j, s, pieces):
        for (a, n) in pieces:
            gather(slot(T.D1, j, s, a, n), by(tab, buf, c0, a, n), n, tkeys + offk(o, a, n), un("D%d_%d" % (j, s), a, n))

    for t in range(R):
        SF, GF, SFK, GFK = T["SF%d" % t], T["GF%d" % t], all3("SF%d" % t), all3("GF%d" % t)
        St, Qt, u = "S%d" % t, "Q%d" % t, t + 1
        if t == 0:
            names(T.E, 0, ["E0a", "E0b"], [(0, 0)])
            link(T.E, EK, T.OFF, 0, 0, [(2, 1), (0, 2)])
            link(T.E, EK, T.OFF, 32, 1, [(1, 3)])
        else:
            spread(T.XF, "XF", t - 1, T["LW%d" % t], 0, ["LW%d" % t])
            link(T.E, EK, T.EXW, 32 * t, None, [(2, 0)])
            link(T.E, EK, T.OFF, 0, 0, [(2, 1)])
            link(T.E, EK, T.OFF, 32, 1, [(1, 3), (2, 2)])
        for j in range(3):
            link(T.XF, XFK, T.OFF, 32 * (3 + j), 3 + j, [(0 if t == 0 else 2, 4 + j)])
        if t == 0:
            dma(["LXh", "LXl"], XFK, [(T.XF[4 + y:112:16, :], T.LX[16:128, 96 * y:96 * y + 96]) for y in (0, 1)]
                + [(T.XF[116 + y:117 + y, :], T.LX[0:16, 96 * y:96 * y + 96]) for y in (0, 1)], 5e4)
        if t == 1:
            k0, k2 = ["XF0a", "XF0b"], ["XF2a", "XF2b"]
            dma(k0 + k2, k0 + k2, [p for y in (0, 1) for p in (
                (T.XF[6 + y:112:16, 0:LR], T.XF[20 + y:128:16, 0:LR]), (T.XF[118 + y:119 + y, 0:LR], T.XF[4 + y:5 + y, 0:LR]),
                (T.XF[4 + y:96:16, 2 * LR:V], T.XF[32 + y:128:16, 2 * LR:V]), (T.XF[100 + y:128:16, 2 * LR:V], T.XF[y:32:16, 2 * LR:V]))], 3e4)
            dma(k0, k0, [(T.XF[4 + y::16, 0:LR], T.XF[6 + y::16, 0:LR]) for y in (0, 1)], 2e4)
        fetch(GF, GFK, T.OFF, 32 * 6, 6, 0, 0, CHAINS)
        for j, o in enumerate((4, 3, 2, 1, 0, None), 1):
            s, sk, g, gk = (SF, SFK, GF, GFK) if j < 3 else (T.S, all3("S"), T.NG, all3("NG"))
            buf, c0 = (T.OFF, 32 * o) if o is not None else (T.EXW, 32 * t)
            fetch(g, gk, buf, c0, o, j, 1, WHOLE)
            fetch(s, sk, buf, c0, o, j, 2, WHOLE if t and o is None else HALVES)
        act(LR, ["NG%d" % t], un("D7_1"), slot(T.D1, 7, 1, 0, LR), blk(T.NG, t), ACT.Identity)
        act(LR, [St], un("D7_2"), slot(T.D1, 7, 2, 0, LR), blk(T.S, t), ACT.Identity)
        for j in range(8):
            for (a, n) in CHAINS:
                dk = [un("D%d_%d" % (j, s), a, n) for s in range(3)]
                yk, y = un("Y", a, n), slot(T.Y, 0, 2, a, n)
                if j == 0:
                    d = slot(T.D1, 0, 1, a, n)
                    tt(d, by(GF, T.OFF, 160, a, n), slot(T.D1, 0, 0, a, n), ALU.subtract, GFK + offk(5, a, n) + dk[0], dk[1], n, FUSED)
                    tt(y, by(SF, T.OFF, 160, a, n), d, ALU.add, SFK + offk(5, a, n) + dk[1], yk, n, FUSED)
                else:
                    scan(T.Y[:, 3 * a:3 * (a + n)], T.D0[:, 3 * a:3 * (a + n)], T.D1[:, j * V + 3 * a:j * V + 3 * (a + n)],
                         ["D0c0", "D0c2"] + un("D0s", a, n) + dk[0] + dk[1] + dk[2], yk, 3 * n)
                if j < 7:
                    act(n, yk, un("D0s", a, n), slot(T.D0, 0, 1, a, n), y, ACT.Square)
                    act(n, yk, un("D%d_0" % (j + 1), a, n), slot(T.D1, j + 1, 0, a, n), y, ACT.Identity, bias=1.5, scale=-1.0)
        join([], [St])
        join([], [Qt])
        for (a, n) in CHAINS:
            yk, y, c = un("Y", a, n), slot(T.Y, 0, 2, a, n), 2 * (t * LR + a)
            act(n, yk + [St], un(St, a, n), blk(T.S, t, a, n), y, ACT.Identity)
            act(n, yk, un("SQ%d" % t, a, n), pair(T.SQ, t, a, n, 0), y, ACT.Square)
            act(n, yk, un("VL", a, n), pair(T.SQ, t, a, n, 1), y, ACT.Square, bias=1.0, scale=-1.0)
            scan(T.Q[:, c:c + 2 * n], T.DQ[:, 0:2 * n], T.SQ[:, c:c + 2 * n], ["DQ", Qt] + un("SQ%d" % t, a, n) + un("VL", a, n), un(Qt, a, n), 2 * n)
        join(un(St), [St])
        join(un(Qt), [Qt])
        if t < R - 1:
            snd("S%d" % u, [St], 3.0, 10.0)
            dma(["LS%d" % u], ["SF%d%d" % (u, t)], rot(T["SF%d" % u], t * LR, T["LS%d" % u], 0, LR, u), 4e5)
        dma([St] + (["leftS%d" % u] if t < R - 1 else []), [], [(blk(T.ys, t), blk(T.S, t))], 2.6e5)
        QK = all3("Q") + ["NBW%d" % t]
        tt(blk(T.M, 0), by(T.Q, T.NBW, 160 * t, 0, LR), blk(T.W0, t), ALU.mult, QK + ["W0"], ["M0"], LR, FUSED)
        for k in range(1, 5):
            w, wk = bank(k - 1), "pb%d" % (k - 1)
            pe(LR, ["WS", "TR"], k - 1, lambda q, e, w=w, k=k, t=t: q.matmul(w, T.WS[:, 128 * k:128 * k + 128], blk(T.TR, t), True, True))
            gather(blk(T.QG, k), by(T.Q, T.NBW, 160 * t + 32 * k, 0, LR), LR, QK, ["QG%d" % k])
            tt(w, w, blk(T.QG, k), ALU.mult, [wk, "QG%d" % k], [wk], LR)
            tt(blk(T.M, k) if k < 4 else bank(4), w, blk(T.M, k - 1), ALU.max, [wk, "M%d" % (k - 1)], ["M%d" % k if k < 4 else "pb4"], LR)
        tt(blk(T.AV, 3), blk(T.M, 3), bank(3), ALU.is_ge, ["pb3", "M3"], ["AV3"], LR)
        for k in (2, 0, 1):
            tt(blk(T.AV, k), blk(T.M, k), bank(4), ALU.is_ge, ["pb4", "M%d" % k], ["AV%d" % k], LR)
        for x in (1, 0):
            pe(64, ["ONE", "CK%d" % x], 5 + x, lambda q, e, x=x: q.matmul(bank(5 + x, 64), T.ONE[0:1, 0:128], T.CK[:, 64 * x:64 * x + 64], True, False))
            wrap(lambda r, x=x: T.AV[:, 2 * x * LR + r:2 * (x + 1) * LR:16], 3, 5 + x, 64, ["AV%d" % (2 * x), "AV%d" % (2 * x + 1)], False)
        c = lambda a, b, s=1, t=t: T.CODE[:, 6 * t + a:6 * t + b:s, :]
        ck = lambda *ks, t=t: ["CODE%d_%d" % (t, k) for k in ks]
        tt(c(3, 5), bank(6, 64), T.NB[:, t, 64:128], ALU.add, ["pb6", "NB"], ck(3, 4), 64)
        tt(c(4, 6), c(4, 6), bank(6, 64), ALU.subtract, ["pb6"] + ck(4, 5), ck(4, 5), 64)
        tt(c(2, 3), c(4, 5), c(5, 6), ALU.max, ck(4, 5), ck(2), 32, 2)
        if t < R - 1:
            act(LR, [St], ["pb7"], bank(7), blk(T.S, t), ACT.Identity, bias=-1.5)
            tt(blk(T.NG, t), bank(7), pair(T.SQ, t, 0, LR, 0), ALU.mult, ["pb7", "AV1"] + un("SQ%d" % t), ["NG%d" % t], LR)
        tt(c(0, 2), bank(5, 64), T.NB[:, t, 0:64], ALU.add, ["pb5", "NB", "NG%d" % t], ck(0, 1), 64)
        tt(c(1, 4, 2), c(1, 4, 2), bank(5, 64), ALU.subtract, ["pb5"] + ck(1, 3), ck(1, 3), 64)
        tt(T.MX[:, :], c(0, 2), c(2, 4), ALU.max, ck(0, 1, 2, 3), ["MX"], 64, 2)
        tt(T.MI[:, 0:32], T.MX[:, 0:32], T.MX[:, 32:64], ALU.max, ["MX"], ["MI0"], 32, 2)
        ts(T.MI[:, 32:64], T.MI[:, 0:32], 2047, ALU.bitwise_and, ["MI0"], ["MI1"], 32)
        cp(T.XO[:, :], T.MI[:, 32:64], ["MI1"], ["XO"], 32)
        if t < R - 1:
            pe(256, ["XO", "I2"], 6, lambda q, e, u=u: q.matmul(bank(6, 32), T.I2[:, 16 * u:16 * u + 128], T.XO[:, :], True, True))
            cp(T["RU%d" % u][:, :], bank(6, 32), ["pb6"], ["RU%d" % u], 32)
            snd("W%d" % u, ["RU%d" % u], 1.5, 5.5)
            cp(T.NW[:, :], T.MI[:, 32:64], ["MI1"], ["NW"], 32)
            spread(T.E, "E", t, T.NW, 0, ["NW"])
            ntab(T["LS%d" % u], T.LG, 0, ["LS%d" % u], ["LG"], 0, blk(T.TF, 0), ["TF0"])
            dma(["LG"], ["GF%d%d" % (u, t)], rot(T["GF%d" % u], t * LR, T.LG, 0, LR, u), 4e5)
            if t == 0:
                dma(["LG", "GF10"], ["GF20"], rot(T.GF2, 0, T.LG, 0, LR, 2), 2.6e5)
                dma(["LS1", "GF10"], ["SF20"], rot(T.SF2, 0, T.LS1, 0, LR, 2), 2.6e5)
        vec(32, 1, ["XO"], ["XT%d" % t], lambda q, e, t=t: q.transpose(T.XT[:, 32 * t:32 * t + 32], T.XO[:, :]))
        for q in (0, 1):
            dma(["XT%d" % t], [], [(T.yx[q::2, t * LR:t * LR + LR], T.XT[:, 32 * t + 16 * q:32 * t + 16 * q + 16])], 2e4,
                eng="A" if q and t == R - 1 else "S")
    return ops


def edges(ops):
    last, readers, deps = {}, {}, []
    for i, o in enumerate(ops):
        d = {}
        for k in o["rd"]:
            if k in last:
                d[last[k]] = True
            if k[:2] == "pb":
                for j in readers.get(k, []):
                    if ops[j]["eng"] != o["eng"] or len(o["eng"]) > 1:
                        d.setdefault(j, False)
        for k in o["wr"]:
            if k in last:
                d[last[k]] = True
            for j in readers.get(k, []):
                d[j] = True
        d.pop(i, None)
        deps.append(d)
        for k in o["rd"]:
            readers.setdefault(k, []).append(i)
        for k in o["wr"]:
            last[k] = i
            readers[k] = []
    return deps


def run(seq, a, eng, dl, dur, lat, sy, fin, end):
    free = {"V": 0.0, "A": 0.0, "P": 0.0, "G": 0.0, "S": 0.0, None: 0.0}
    for i in seq[:a]:
        free[eng[i]] = end[i]
    for i in seq[a:]:
        r = 0.0
        for j in dl[i]:
            if fin[j] > r:
                r = fin[j]
        e = eng[i]
        if e is not None:
            r += sy
            if free[e] > r:
                r = free[e]
            r += dur[i][e]
            free[e] = r
        end[i] = r
        fin[i] = r + lat[i]
    return max(fin) + OPT["PULL"] * sum(fin) / len(fin)


def pack(win, ops, dl, succ, prio, pen, free, fin, eng, back=False):
    sy, inw = PAR["sy"], set(win)
    busy = {e: [(0.0, free[e])] for e in "VAPGS"}
    left = {i: sum(j in inw for j in dl[i]) for i in win}
    todo = [i for i in win if not left[i]]
    start = {}
    while todo:
        i = min(todo, key=prio.get)
        todo.remove(i)
        o = ops[i]
        r = max([fin[j] for j in dl[i]] + [0.0])
        if not o["eng"]:
            start[i], fin[i] = r, r + o["lat"]
        else:
            best = None
            for e in o["eng"]:
                s, du, k = r + sy + (o["lat"] if back else 0.0), o["dur"][e], 0
                for k, (x, y) in enumerate(busy[e] + [(1e9, 1e9)]):
                    if s + du <= x:
                        break
                    s = max(s, y)
                w = s + du + (pen if e == "V" else 0.0)
                if best is None or w < best[0]:
                    best = (w, s, e, k)
            w, s, e, k = best
            start[i], eng[i], fin[i] = s, e, s + o["dur"][e] + (0.0 if back else o["lat"])
            busy[e].insert(k, (s, s + o["dur"][e]))
        for j in succ[i]:
            if j in inw:
                left[j] -= 1
                if not left[j]:
                    todo.append(j)
    return sorted(win, key=lambda i: (start[i], i))


def arrange(T):
    sets = []
    for p in PARS:
        PAR.update(p)
        ops = build(T)
        sets.append(([o["dur"] for o in ops], [o["lat"] for o in ops], p["sy"]))
    PAR.update(PARS[0])
    ops = build(T)
    deps = edges(ops)
    n = len(ops)
    dl = [list(d) for d in deps]
    succ = [[] for o in ops]
    rank = [0.0] * n
    for i in range(n - 1, -1, -1):
        o = ops[i]
        rank[i] += min([o["dur"][e] for e in o["eng"]] or [0.0]) + o["lat"]
        for j in dl[i]:
            succ[j].append(i)
            rank[j] = max(rank[j], rank[i] + PAR["sy"])
    x = [OPT["SEED"]]

    def rnd():
        x[0] = (x[0] * 6364136223846793005 + 1442695040888963407) % (1 << 64)
        return (x[0] >> 33) / float(1 << 31)

    first = [i for i in range(n) if ops[i]["x"] is True]
    eng = [None] * n
    seq = pack(list(range(n)), ops, dl, succ, {i: i - 1e6 if i in first else -rank[i] for i in range(n)}, 0.0,
               dict.fromkeys("VAPGS", 0.0), [0.0] * n, eng)
    seq = first + [i for i in seq if i not in first]
    times = [([0.0] * n, [0.0] * n) for s in sets]
    base = [run(seq, 0, eng, dl, *s, *t) for s, t in zip(sets, times)]
    weight = [w / b for w, b in zip(OPT["WEIGHT"], base)]
    best, now = sum(OPT["WEIGHT"]), base[0]
    keep = (best, seq, eng)
    for it in range(OPT["TRIES"]):
        a = len(first) + int(rnd() * (n - len(first) - 10))
        win = seq[a:a + 10 + int(rnd() * OPT["WIN"])]
        fin, end = times[0]
        free = dict.fromkeys("VAPGS", 0.0)
        for i in seq[:a]:
            free[eng[i]] = end[i]
        amp, mix = OPT["AMP"] * rnd(), rnd() < 0.3
        prio = {i: (-rank[i] if mix else end[i]) + amp * rnd() for i in win}
        en = list(eng)
        if rnd() < OPT["BACK"]:
            top = max(fin)
            rev = [top - end[i] + (ops[i]["dur"][eng[i]] if eng[i] else 0.0) for i in range(n)]
            after = dict.fromkeys("VAPGS", 0.0)
            for i in reversed(seq[a + len(win):]):
                after[eng[i]] = rev[i]
            pack(win, ops, succ, dl, {i: amp * rnd() - fin[i] for i in win}, OPT["PEN"] * rnd() * rnd(), after, rev, list(eng), True)
            prio = {i: amp * rnd() * 0.5 - rev[i] for i in win}
        sq = seq[:a] + pack(win, ops, dl, succ, prio, OPT["PEN"] * rnd() * rnd(), free, list(fin), en) + seq[a + len(win):]
        limit = best + OPT["HEAT"] * (1.0 - it / OPT["TRIES"]) * rnd() * rnd()
        tm, vs = [], []
        for st, t in zip(sets, times):
            tm.append((list(t[0]), list(t[1])))
            vs.append(run(sq, a, en, dl, *st, *tm[-1]))
            if vs[0] > now + 0.5:
                break
        s = sum(w * v for w, v in zip(weight, vs))
        if len(vs) == len(sets) and s <= limit:
            best, now, eng, times = s, vs[0], en, tm
            pos = {j: k for k, j in enumerate(sq)}
            seq = first + sorted(sq[len(first):], key=lambda j: (tm[0][1][j] - (ops[j]["dur"][en[j]] if en[j] else 0.0), pos[j]))
            if s < keep[0]:
                keep = (s, seq, eng)
    return deps, keep[1], keep[2]


PLAN = {}


def rank_program(g, core, T, topo):
    rank = T.rank_of(core)
    if rank is None:
        relay_program(g, core, T, topo)
        return
    n = len(T.cores)
    dst, src = T.cores[(rank - 1) % n], T.cores[(rank + 1) % n]
    if not PLAN:
        PLAN["plan"] = arrange(T)
    ops = build(T)
    deps, seq, eng = PLAN["plan"]
    Qs = {"V": g.vector, "A": g.scalar, "P": g.tensor, "G": g, "S": g.sync}
    clock = {e: {} for e in Qs}
    count = {}
    tok = {}
    ndma = [0]
    for i in seq:
        o, e = ops[i], eng[i]
        if o["kind"] == "a":
            m = o["x"]
            c = arrivals(T, topo, src, core, m)
            count["a" + m] = c
            tok[i] = [("a" + m, c, {}, None)]
            continue
        if o["kind"] == "j":
            top = {}
            for j in deps[i]:
                for x in tok[j]:
                    if x[0] not in top or top[x[0]][1] < x[1]:
                        top[x[0]] = x
            tok[i] = list(top.values())
            continue
        need = {}
        for j, hard in deps[i].items():
            if o["kind"] == "s" and ops[j]["kind"] == "s":
                continue
            for x in tok[j]:
                if x[3] == e and not hard:
                    continue
                if x[0] not in need or need[x[0]][1] < x[1]:
                    need[x[0]] = x
        ck = clock[e]
        todo = sorted(need.values(), key=lambda x: -len(x[2]))
        for (s, c, known, qq) in todo:
            if ck.get(s, 0) < c:
                Qs[e].wait_ge(T.sem[s], c)
                ck[s] = c
                for s2, c2 in known.items():
                    if ck.get(s2, 0) < c2:
                        ck[s2] = c2
        if o["kind"] == "c":
            s = "c" + e
            o["fn"](Qs[e], e).then_inc(T.sem[s], 1)
            count[s] = count.get(s, 0) + 1
            tok[i] = [(s, count[s], dict(ck), e)]
        elif o["kind"] == "d":
            s = "d%d" % ndma[0]
            ndma[0] += 1
            for (a, b) in o["fn"]:
                Qs[e].dma_start(a, b).then_inc(T.sem[s], 16)
            count[s] = 16 * len(o["fn"])
            tok[i] = [(s, count[s], dict(ck), None)]
        else:
            s = "l" + o["x"]
            count[s] = send(g, T, topo, core, dst, o["x"])
            tok[i] = [(s, count[s], dict(ck), None)]
    for s, c in count.items():
        if clock["G"].get(s, 0) < c:
            g.wait_ge(T.sem[s], c)
